import numpy as np
import ml_dtypes


def mxq(x, axis, fmt="e4m3"):
    dtype, down = {"e4m3": (ml_dtypes.float8_e4m3fn, 7), "e5m2": (ml_dtypes.float8_e5m2, 14)}[fmt]
    v = np.moveaxis(np.asarray(x, np.float32).astype(ml_dtypes.bfloat16).astype(np.float64), axis, -1)
    blocks = v.reshape(v.shape[:-1] + (-1, 32))
    amax = np.abs(blocks).max(-1, keepdims=True)
    byte = np.maximum(np.where(amax > 0, np.frexp(amax)[1] - 1 + 127, 0) - down, 1)
    scale = np.exp2(byte - 127.0)
    codes = (blocks / scale).astype(np.float32).astype(dtype).astype(np.float64)
    return np.moveaxis((codes * scale).reshape(v.shape), -1, axis)


WIDE = False


def mx_kscale(k):
    if not WIDE:
        return np.ones(k)
    levels = np.array([10, -10, 5, -5, 0])
    if k % 512:
        return np.exp2(np.random.permutation(np.resize(levels, k // 32))).repeat(32)
    a = np.empty((k // 512, 16))
    for p in range(k // 512):
        a[p, :8] = np.random.permutation(np.resize(levels, 8))
        for g in range(8):
            far = levels[np.abs(levels - a[p, g]) >= 10]
            a[p, g + 8] = far[np.random.randint(len(far))]
    return np.exp2(a.ravel()).repeat(32)


def f64(x):
    return np.asarray(x).astype(np.float64)


def striped(idx):
    return np.tile(idx.reshape(-1, 16).T, (8, 1)).astype(np.uint16)


def unstriped(offs):
    return offs[:16].T.reshape(-1).astype(np.int64)


E2M1 = np.array([0.0, 0.5, 1.0, 1.5, 2.0, 3.0, 4.0, 6.0, -0.0, -0.5, -1.0, -1.5, -2.0, -3.0, -4.0, -6.0])


def pack_weight(w, fmt):
    k, n = w.shape
    w = f64(np.asarray(w, np.float32).astype(ml_dtypes.bfloat16)).reshape(k // 32, 32, n)
    amax = np.abs(w).max(1)
    if fmt == "e4m3":
        byte = np.frexp(amax)[1] - 1 + 127 - 7
    else:
        mant, ex = np.frexp(amax / 6.0)
        byte = np.where(mant > 0.5, ex, ex - 1) + 127
    byte = np.clip(np.where(amax > 0, byte, 1), 1, 254)
    scaled = (w * np.exp2(127.0 - byte)[:, None, :]).reshape(k, n).astype(np.float32)
    by_word = np.ascontiguousarray(scaled.reshape(k // 512, 128, 4, n).transpose(0, 1, 3, 2))
    if fmt == "e4m3":
        words = by_word.astype(ml_dtypes.float8_e4m3fn).view(np.uint8)
    else:
        c = by_word.astype(ml_dtypes.float4_e2m1fn).view(np.uint8) & 0xF
        words = (c[..., 0::2] | (c[..., 1::2] << 4)).reshape(k // 512, 128, 2 * n)
    return np.ascontiguousarray(words), np.ascontiguousarray(byte.astype(np.uint8).reshape(k // 512, 16, n))


def unpack_weight(words, scales, fmt):
    g, _, n = scales.shape
    words = np.ascontiguousarray(words).reshape(g, 128, n, -1)
    if fmt == "e4m3":
        vals = words.view(ml_dtypes.float8_e4m3fn).astype(np.float64)
    else:
        nib = np.empty((g, 128, n, 4), np.uint8)
        nib[..., 0::2] = words & 0xF
        nib[..., 1::2] = words >> 4
        vals = E2M1[nib]
    vals = vals * np.repeat(np.exp2(scales.astype(np.float64) - 127.0), 8, axis=1)[..., None]
    return vals.transpose(0, 1, 3, 2).reshape(g * 512, n)


def gelu(v):
    return 0.5 * v * (1.0 + np.tanh(np.sqrt(2.0 / np.pi) * (v + 0.044715 * v**3)))


def striped8(idx):
    return np.concatenate([v.reshape(-1, 16).T for v in idx]).astype(np.uint16)


def unstriped8(offs):
    return np.stack([offs[16 * g:16 * g + 16].T.reshape(-1) for g in range(8)]).astype(np.int64)


def heads(h, wgt, idx8):
    r = np.arange(h.shape[0])
    return wgt[r // 4 % 128] * h[r[:, None], idx8[r % 512 // 64]]


def bf(x):
    return np.asarray(x, np.float32).astype(ml_dtypes.bfloat16)


def planes(Y):
    n, m = Y.shape
    b = f64(bf(Y)).reshape(n // 32, 32, m)
    amax = np.abs(b).max(1)
    byte = np.clip(np.where(amax > 0, np.frexp(amax)[1] - 1 + 127 - 7, 1), 1, 254)
    codes = (b * np.exp2(127.0 - byte)[:, None, :]).reshape(n, m).astype(np.float32).astype(ml_dtypes.float8_e4m3fn).view(np.uint8)
    words = codes.reshape(n // 512, 128, 4, m).transpose(0, 1, 3, 2)
    return np.ascontiguousarray(words), np.ascontiguousarray(byte.astype(np.uint8).reshape(n // 512, 16, m))


K, T, S, P, H, N = 1024, 2048, 1024, 512, 512, 512

def setup_inputs():
    n = np.random.standard_normal
    s = mx_kscale(K)[:, None]
    u = mx_kscale(H)[:, None]
    freq = np.geomspace(0.01, 0.42, H)[None, :]
    phase = 2.0 * np.pi * freq * np.arange(K)[:, None]
    tab_words, tab_scales = pack_weight(n((K, T)) * s, "e4m3")
    tpl = n((H, N)) / np.sqrt(H) * np.exp(0.8 * n((1, N))) / u
    tpl_words, tpl_scales = pack_weight(tpl, "e2m1")
    return {
        "tab_words": tab_words, "tab_scales": tab_scales,
        "offs": striped(np.random.permutation(T)[:S]),
        "wcos": (np.cos(phase) * np.sqrt(2.0 / K) / s).astype(np.float32),
        "wsin": (np.sin(phase) * np.sqrt(2.0 / K) / s).astype(np.float32),
        "offs2": striped8(np.stack([np.random.permutation(S)[:P] for _ in range(8)])),
        "wgt": np.repeat(np.random.uniform(0.5, 2.0, (8, P)), 16, axis=0).astype(np.float32),
        "gain": (np.exp(0.3 * n(H)) * u[:, 0]).astype(np.float32),
        "tpl_words": tpl_words, "tpl_scales": tpl_scales,
    }

def reference(tab_words, tab_scales, offs, wcos, wsin, offs2, wgt, gain, tpl_words, tpl_scales):
    v = unpack_weight(tab_words, tab_scales, "e4m3")[:, unstriped(offs)]
    re = mxq(f64(wcos), 0, "e4m3").T @ v
    im = mxq(f64(wsin), 0, "e4m3").T @ v
    h = np.sqrt(np.square(re) + np.square(im))
    x = heads(h, f64(wgt), unstriped8(offs2))
    z = f64(gain)[:, None] * np.log1p(x)
    tp = unpack_weight(tpl_words, tpl_scales, "e2m1")
    y = tp.T @ mxq(z, 0, "e4m3")
    words, scales = planes(y)
    return y, words, scales

@@ -1,0 +1,291 @@
+from contextlib import ExitStack
+
+import concourse.mybir as mybir
+from concourse.masks import make_identity
+
+K, T, S, M, H, N = 1024, 2048, 1024, 512, 512, 512
+FLOPS = 2 * (2 * K * H * S) + 2 * H * N * M
+
+F32 = mybir.dt.float32
+BF16 = mybir.dt.bfloat16
+I32 = mybir.dt.int32
+U32 = mybir.dt.uint32
+U16 = mybir.dt.uint16
+U8 = mybir.dt.uint8
+FP8X4 = mybir.dt.float8_e4m3fn_x4
+FP4X4 = mybir.dt.float4_e2m1fn_x4
+ACT = mybir.ActivationFunctionType
+MULT = mybir.AluOpType.mult
+
+P = 128
+PACK = 4
+K_PASS = P * PACK
+PASSES = K // K_PASS
+HALF = H // 2
+BANK = 512
+LIST_COLS = 16
+QUARTER = M // 4
+
+
+def tile_list_pitch_salience_kernel(
+    tc, tab_words, tab_scales, offs, wcos, wsin, offs2, wgt, gain, tpl_words, tpl_scales, out_0, out_1, out_2
+):
+    nc = tc.nc
+    with ExitStack() as ctx:
+        keep = ctx.enter_context(tc.tile_pool(name="keep", bufs=1))
+        psum = ctx.enter_context(tc.psum_pool(name="psum", bufs=1))
+
+        def tile(name, shape, dtype):
+            return keep.tile(shape, dtype, name=name, align_bytes=64)
+
+        def bank(b, shape):
+            return psum.tile(shape, F32, name="bank%d" % b)
+
+        frames = tile("frames", [P, S // LIST_COLS], U16)
+        nc.sync.dma_start(frames[:], offs)
+
+        table_scales = tile("table_scales", [P, T], U8)
+        nc.vector.memset(table_scales[:].bitcast(I32), 0)
+        for q in range(4):
+            nc.sync.dma_start(
+                table_scales[32 * q : 32 * q + 4 * PASSES, :].bitcast(I32),
+                tab_scales[:, 4 * q : 4 * q + 4, :].bitcast(I32),
+            )
+
+        table = [tile("table%d" % a, [P, T], U32) for a in range(PASSES)]
+        chunks = [(w, h) for w in range(2) for h in range(2)]
+        basis = (wcos, wsin)
+        raw = {}
+
+        def load_table(a):
+            nc.sync.dma_start(table[a][:].bitcast(I32), tab_words[a].rearrange("p t i -> p (t i)").bitcast(I32))
+
+        def load_basis(c, a):
+            w, h = chunks[c]
+            raw[c, a] = tile("raw%d_%d" % (c, a), [P, PACK, HALF], F32)
+            rows = basis[w][a * K_PASS : (a + 1) * K_PASS, h * HALF : (h + 1) * HALF]
+            nc.sync.dma_start(raw[c, a][:], rows.rearrange("(p j) c -> p j c", j=PACK))
+
+        load_table(0)
+        load_basis(0, 0)
+        load_basis(0, 1)
+        load_basis(1, 0)
+        load_table(1)
+        load_basis(1, 1)
+        for c in range(2, 4):
+            for a in range(PASSES):
+                load_basis(c, a)
+
+        picks = tile("picks", [P, M // LIST_COLS], U16)
+        nc.sync.dma_start(picks[:], offs2)
+        weight = tile("weight", [P, M], F32)
+        nc.sync.dma_start(weight[:], wgt)
+        gains = tile("gains", [P, PACK], F32)
+        nc.sync.dma_start(gains[:], gain.rearrange("(p i) -> p i", i=PACK))
+        tpl_raw = tile("tpl_raw", [P, 2 * N], U8)
+        nc.sync.dma_start(tpl_raw[:].bitcast(I32), tpl_words[0].bitcast(I32))
+        tpl_raw_scales = tile("tpl_raw_scales", [P, N], U8)
+        nc.vector.memset(tpl_raw_scales[:].bitcast(I32), 0)
+        for q in range(4):
+            nc.sync.dma_start(
+                tpl_raw_scales[32 * q : 32 * q + 4, :].bitcast(I32),
+                tpl_scales[0, 4 * q : 4 * q + 4, :].bitcast(I32),
+            )
+
+        ident = tile("ident", [P, P], F32)
+        make_identity(nc, ident[:])
+
+        got_words = {}
+        got_scales = {}
+
+        def listed(jh):
+            return frames[:, jh * BANK // LIST_COLS : (jh + 1) * BANK // LIST_COLS]
+
+        def gather_scales(jh):
+            got_scales[jh] = tile("got_scales%d" % jh, [P, BANK], U8)
+            nc.vector.tensor_copy(got_scales[jh][:], table_scales[:].indirect(listed(jh)))
+
+        def gather_words(a, jh):
+            got_words[a, jh] = tile("got_words%d_%d" % (a, jh), [P, BANK], U32)
+            nc.vector.tensor_copy(got_words[a, jh][:], table[a][:].indirect(listed(jh)))
+
+        grouped = {}
+        codes = {}
+        scales = {}
+
+        def round_basis(c, a, on_scalar):
+            grouped[c, a] = tile("grouped%d_%d" % (c, a), [P, HALF, PACK], BF16)
+            dst = grouped[c, a][:].rearrange("p (c e) j -> p c j e", e=4)
+            src = raw[c, a][:].rearrange("p j (c e) -> p c j e", e=4)
+            if on_scalar:
+                nc.scalar.copy(dst, src)
+            else:
+                nc.vector.tensor_copy(dst, src)
+
+        def quantise_basis(c, a):
+            codes[c, a] = tile("codes%d_%d" % (c, a), [P, HALF], U32)
+            scales[c, a] = tile("scales%d_%d" % (c, a), [P, HALF], U8)
+            nc.vector.quantize_mx(
+                out=codes[c, a][:].bitcast(FP8X4),
+                scales=scales[c, a][:],
+                in_=grouped[c, a][:].rearrange("p c j -> p (c j)"),
+            )
+
+        squares = {(w, g): tile("squares%d_%d" % (w, g), [P, 2, PACK, P], F32) for w in range(2) for g in range(4)}
+
+        accs = {}
+
+        def products(c, a):
+            w, h = chunks[c]
+            for g in range(4):
+                if a == 0:
+                    accs[c, g] = bank(4 * (c % 2) + g, [P, 2, HALF])
+                for u in range(2):
+                    jh, cols = g // 2, slice((2 * (g % 2) + u) * P, (2 * (g % 2) + u + 1) * P)
+                    nc.tensor.matmul_mx(
+                        out=accs[c, g][:, u, :],
+                        lhsT=got_words[a, jh][:, cols].bitcast(FP8X4),
+                        lhsT_scale=got_scales[jh][4 * a : P, cols],
+                        rhs=codes[c, a][:].bitcast(FP8X4),
+                        rhs_scale=scales[c, a][:],
+                        start=(a == 0 and u == 0),
+                        stop=(a == PASSES - 1 and u == 1),
+                    )
+                if a == PASSES - 1:
+                    nc.scalar.activation(
+                        squares[w, g][:, :, :, h * 64 : (h + 1) * 64],
+                        accs[c, g][:].rearrange("j u (p i) -> j u i p", i=PACK),
+                        ACT.Square,
+                    )
+
+        gather_words(0, 0)
+        gather_words(0, 1)
+        gather_scales(0)
+        gather_scales(1)
+        for c, a in ((0, 0), (0, 1), (1, 0)):
+            round_basis(c, a, True)
+            quantise_basis(c, a)
+        products(0, 0)
+        products(1, 0)
+        gather_words(1, 0)
+        gather_words(1, 1)
+        products(0, 1)
+        round_basis(1, 1, False)
+        round_basis(2, 0, False)
+        quantise_basis(1, 1)
+        products(1, 1)
+        round_basis(2, 1, False)
+        quantise_basis(2, 0)
+        products(2, 0)
+        round_basis(3, 0, False)
+        quantise_basis(2, 1)
+        products(2, 1)
+        round_basis(3, 1, False)
+        quantise_basis(3, 0)
+        products(3, 0)
+        quantise_basis(3, 1)
+        products(3, 1)
+
+        tpl = tile("tpl", [P, PACK, P, 2], U8)
+        nc.vector.tensor_copy(tpl[:], tpl_raw[:].rearrange("p (m t b) -> p t m b", t=PACK, b=2))
+        tpl_sc = tile("tpl_sc", [P, PACK, P], U8)
+        nc.vector.tensor_copy(tpl_sc[:], tpl_raw_scales[:].rearrange("p (m t) -> p t m", t=PACK))
+
+        mags = [tile("mag%d" % i, [P, S], F32) for i in range(PACK)]
+        for i in range(PACK):
+            for jh in range(2):
+                power = bank(2 * i + jh, [P, 4, P])
+                for w in range(2):
+                    for b in range(4):
+                        nc.tensor.matmul(
+                            power[:, b, :],
+                            squares[w, 2 * jh + b // 2][:, b % 2, i, :],
+                            ident[:],
+                            start=(w == 0 and b == 0),
+                            stop=(w == 1 and b == 3),
+                            is_transpose=True,
+                        )
+                nc.scalar.activation(
+                    mags[i][:, jh * BANK : (jh + 1) * BANK], power[:].rearrange("p b j -> p (b j)"), ACT.Sqrt
+                )
+
+        x = [tile("x%d" % mh, [P, PACK, M // 2], F32) for mh in range(2)]
+
+        def pick(i, mh):
+            cols = slice(mh * (M // 2), (mh + 1) * (M // 2))
+            entries = picks[:, mh * (M // 2) // LIST_COLS : (mh + 1) * (M // 2) // LIST_COLS]
+            nc.vector.tensor_tensor(x[mh][:, i, :], mags[i][:].indirect(entries), weight[:, cols], MULT)
+
+        for i, mh in ((0, 0), (0, 1), (1, 0), (1, 1), (2, 0), (3, 0), (2, 1), (3, 1)):
+            pick(i, mh)
+
+        z_codes = tile("z_codes", [P, M], U32)
+        z_scales = tile("z_scales", [P, M], U8)
+        y_codes = tile("y_codes", [P, M], U32)
+        y_scales = tile("y_scales", [P, M], U8)
+        y_rows = out_0.rearrange("(p t) m -> p t m", t=PACK)
+        y_words = out_1[0].rearrange("p m t -> p (m t)").bitcast(I32)
+        z = {}
+        y = {}
+        sums = {}
+
+        def log_gain(u):
+            logs = tile("logs%d" % u, [P, QUARTER, PACK], F32)
+            part = x[u // 2][:, :, (u % 2) * QUARTER : (u % 2 + 1) * QUARTER]
+            nc.scalar.activation(
+                logs[:].rearrange("p (c e) i -> p c i e", e=4),
+                part.rearrange("p i (c e) -> p c i e", e=4),
+                ACT.Ln,
+                bias=1.0,
+            )
+            z[u] = tile("z%d" % u, [P, QUARTER, PACK], BF16)
+            nc.vector.tensor_tensor(z[u][:], logs[:], gains[:].unsqueeze(1).to_broadcast([P, QUARTER, PACK]), MULT)
+
+        def salience(u):
+            cols = slice(u * QUARTER, (u + 1) * QUARTER)
+            nc.vector.quantize_mx(
+                out=z_codes[:, cols].bitcast(FP8X4), scales=z_scales[:, cols], in_=z[u][:].rearrange("p m i -> p (m i)")
+            )
+            sums[u] = bank(u, [P, PACK, QUARTER])
+            for t in range(PACK):
+                nc.tensor.matmul_mx(
+                    out=sums[u][:, t, :],
+                    lhsT=tpl[:, t, :, :].rearrange("p m b -> p (m b)").bitcast(FP4X4),
+                    lhsT_scale=tpl_sc[:, t, :],
+                    rhs=z_codes[:, cols].bitcast(FP8X4),
+                    rhs_scale=z_scales[:, cols],
+                    start=True,
+                    stop=True,
+                )
+
+        def hand_out(u):
+            cols = slice(u * QUARTER, (u + 1) * QUARTER)
+            y[u] = tile("y%d" % u, [P, PACK, QUARTER], F32)
+            nc.scalar.copy(y[u][:], sums[u][:])
+            nc.sync.dma_start(y_rows[:, :, cols], y[u][:])
+            rounded = tile("rounded%d" % u, [P, QUARTER, PACK], BF16)
+            nc.vector.tensor_copy(
+                rounded[:].rearrange("p (c e) t -> p c t e", e=4), y[u][:].rearrange("p t (c e) -> p c t e", e=4)
+            )
+            nc.vector.quantize_mx(
+                out=y_codes[:, cols].bitcast(FP8X4), scales=y_scales[:, cols], in_=rounded[:].rearrange("p m t -> p (m t)")
+            )
+
+        log_gain(0)
+        log_gain(1)
+        salience(0)
+        log_gain(2)
+        salience(1)
+        log_gain(3)
+        salience(2)
+        hand_out(0)
+        salience(3)
+        hand_out(1)
+        nc.sync.dma_start(y_words[:, 0 : M // 2], y_codes[:, 0 : M // 2].bitcast(I32))
+        hand_out(2)
+        hand_out(3)
+        nc.sync.dma_start(y_words[:, M // 2 : M], y_codes[:, M // 2 : M].bitcast(I32))
+        for q in range(4):
+            nc.scalar.dma_start(
+                out_2[0, 4 * q : 4 * q + 4, :].bitcast(I32), y_scales[32 * q : 32 * q + 4, :].bitcast(I32)
+            )

@@ -16,15 +16,17 @@ FP8X4 = mybir.dt.float8_e4m3fn_x4
 FP4X4 = mybir.dt.float4_e2m1fn_x4
 ACT = mybir.ActivationFunctionType
 MULT = mybir.AluOpType.mult
+ADD = mybir.AluOpType.add
 
 P = 128
 PACK = 4
 K_PASS = P * PACK
 PASSES = K // K_PASS
-HALF = H // 2
 BANK = 512
 LIST_COLS = 16
 QUARTER = M // 4
+TURNED = (2, 3)
+COS, SIN = 0, 1
 
 
 def tile_list_pitch_salience_kernel(
@@ -38,8 +40,8 @@ def tile_list_pitch_salience_kernel(
         def tile(name, shape, dtype):
             return keep.tile(shape, dtype, name=name, align_bytes=64)
 
-        def bank(b, shape):
-            return psum.tile(shape, F32, name="bank%d" % b)
+        def bank(b):
+            return psum.tile([P, BANK], F32, name="bank%d" % b)
 
         frames = tile("frames", [P, S // LIST_COLS], U16)
         nc.sync.dma_start(frames[:], offs)
@@ -52,29 +54,33 @@ def tile_list_pitch_salience_kernel(
                 tab_scales[:, 4 * q : 4 * q + 4, :].bitcast(I32),
             )
 
+        warm = tile("warm", [P, 2], F32)
+        nc.vector.memset(warm[:, 0:1], 1.0)
+        nc.scalar.activation(warm[:, 1:2], warm[:, 0:1], ACT.Sqrt)
+
         table = [tile("table%d" % a, [P, T], U32) for a in range(PASSES)]
-        chunks = [(w, h) for w in range(2) for h in range(2)]
         basis = (wcos, wsin)
         raw = {}
 
         def load_table(a):
             nc.sync.dma_start(table[a][:].bitcast(I32), tab_words[a].rearrange("p t i -> p (t i)").bitcast(I32))
 
-        def load_basis(c, a):
-            w, h = chunks[c]
-            raw[c, a] = tile("raw%d_%d" % (c, a), [P, PACK, HALF], F32)
-            rows = basis[w][a * K_PASS : (a + 1) * K_PASS, h * HALF : (h + 1) * HALF]
-            nc.sync.dma_start(raw[c, a][:], rows.rearrange("(p j) c -> p j c", j=PACK))
+        def load_basis(w, a, c0, c1):
+            raw[w, a, c0] = tile("raw%d_%d_%d" % (w, a, c0), [P, PACK, c1 - c0], F32)
+            rows = basis[w][a * K_PASS : (a + 1) * K_PASS, c0:c1]
+            nc.sync.dma_start(raw[w, a, c0][:], rows.rearrange("(p j) c -> p j c", j=PACK))
 
+        load_basis(COS, 0, 0, H // 2)
+        load_basis(COS, 0, H // 2, H)
+        tpl_raw = tile("tpl_raw", [P, 2 * N], U8)
+        nc.sync.dma_start(tpl_raw[:].bitcast(I32), tpl_words[0].bitcast(I32))
         load_table(0)
-        load_basis(0, 0)
-        load_basis(0, 1)
-        load_basis(1, 0)
+        load_basis(COS, 1, 0, H // 2)
+        load_basis(COS, 1, H // 2, H)
         load_table(1)
-        load_basis(1, 1)
-        for c in range(2, 4):
-            for a in range(PASSES):
-                load_basis(c, a)
+        load_basis(SIN, 0, 0, H)
+        load_basis(SIN, 1, 0, H // 2)
+        load_basis(SIN, 1, H // 2, H)
 
         picks = tile("picks", [P, M // LIST_COLS], U16)
         nc.sync.dma_start(picks[:], offs2)
@@ -82,8 +88,6 @@ def tile_list_pitch_salience_kernel(
         nc.sync.dma_start(weight[:], wgt)
         gains = tile("gains", [P, PACK], F32)
         nc.sync.dma_start(gains[:], gain.rearrange("(p i) -> p i", i=PACK))
-        tpl_raw = tile("tpl_raw", [P, 2 * N], U8)
-        nc.sync.dma_start(tpl_raw[:].bitcast(I32), tpl_words[0].bitcast(I32))
         tpl_raw_scales = tile("tpl_raw_scales", [P, N], U8)
         nc.vector.memset(tpl_raw_scales[:].bitcast(I32), 0)
         for q in range(4):
@@ -109,129 +113,167 @@ def tile_list_pitch_salience_kernel(
             got_words[a, jh] = tile("got_words%d_%d" % (a, jh), [P, BANK], U32)
             nc.vector.tensor_copy(got_words[a, jh][:], table[a][:].indirect(listed(jh)))
 
-        grouped = {}
-        codes = {}
-        scales = {}
+        keys = [(w, a) for w in range(2) for a in range(PASSES)]
+        grouped = {(COS, a): tile("grouped%d" % a, [P, PACK, P, PACK], BF16)[:] for a in range(PASSES)}
+        codes = {k: tile("codes%d_%d" % k, [P, H], U32) for k in keys}
+        scales = {k: tile("scales%d_%d" % k, [P, H], U8) for k in keys}
 
-        def round_basis(c, a, on_scalar):
-            grouped[c, a] = tile("grouped%d_%d" % (c, a), [P, HALF, PACK], BF16)
-            dst = grouped[c, a][:].rearrange("p (c e) j -> p c j e", e=4)
-            src = raw[c, a][:].rearrange("p j (c e) -> p c j e", e=4)
-            if on_scalar:
-                nc.scalar.copy(dst, src)
-            else:
-                nc.vector.tensor_copy(dst, src)
+        def round_basis(w, a, c0, c1, copy, first=None):
+            first = c0 if first is None else first
+            dst = grouped[w, a][:, :, c0 // PACK : c1 // PACK, :].rearrange("p t m j -> p m j t")
+            copy(dst, raw[w, a, first][:, :, c0 - first : c1 - first].rearrange("p j (m t) -> p m j t", t=PACK))
 
-        def quantise_basis(c, a):
-            codes[c, a] = tile("codes%d_%d" % (c, a), [P, HALF], U32)
-            scales[c, a] = tile("scales%d_%d" % (c, a), [P, HALF], U8)
+        def quantise_basis(w, a, t0, t1):
             nc.vector.quantize_mx(
-                out=codes[c, a][:].bitcast(FP8X4),
-                scales=scales[c, a][:],
-                in_=grouped[c, a][:].rearrange("p c j -> p (c j)"),
+                out=codes[w, a][:, t0 * P : t1 * P].bitcast(FP8X4),
+                scales=scales[w, a][:, t0 * P : t1 * P],
+                in_=grouped[w, a][:, t0:t1, :, :].rearrange("p t m j -> p (t m j)"),
             )
 
-        squares = {(w, g): tile("squares%d_%d" % (w, g), [P, 2, PACK, P], F32) for w in range(2) for g in range(4)}
-
         accs = {}
+        squares = {}
 
-        def products(c, a):
-            w, h = chunks[c]
-            for g in range(4):
-                if a == 0:
-                    accs[c, g] = bank(4 * (c % 2) + g, [P, 2, HALF])
-                for u in range(2):
-                    jh, cols = g // 2, slice((2 * (g % 2) + u) * P, (2 * (g % 2) + u + 1) * P)
+        def product(w, i, jh, a, b):
+            bins = slice(i * P, (i + 1) * P)
+            if a == 0:
+                accs[w, i, jh] = bank(b)
+            acc = accs[w, i, jh]
+            if i in TURNED:
+                for u in range(4):
+                    cols = slice(u * P, (u + 1) * P)
                     nc.tensor.matmul_mx(
-                        out=accs[c, g][:, u, :],
+                        out=acc[:, cols],
                         lhsT=got_words[a, jh][:, cols].bitcast(FP8X4),
                         lhsT_scale=got_scales[jh][4 * a : P, cols],
-                        rhs=codes[c, a][:].bitcast(FP8X4),
-                        rhs_scale=scales[c, a][:],
+                        rhs=codes[w, a][:, bins].bitcast(FP8X4),
+                        rhs_scale=scales[w, a][:, bins],
                         start=(a == 0 and u == 0),
-                        stop=(a == PASSES - 1 and u == 1),
+                        stop=(a == PASSES - 1 and u == 3),
                     )
-                if a == PASSES - 1:
-                    nc.scalar.activation(
-                        squares[w, g][:, :, :, h * 64 : (h + 1) * 64],
-                        accs[c, g][:].rearrange("j u (p i) -> j u i p", i=PACK),
-                        ACT.Square,
-                    )
-
-        gather_words(0, 0)
-        gather_words(0, 1)
-        gather_scales(0)
-        gather_scales(1)
-        for c, a in ((0, 0), (0, 1), (1, 0)):
-            round_basis(c, a, True)
-            quantise_basis(c, a)
-        products(0, 0)
-        products(1, 0)
-        gather_words(1, 0)
-        gather_words(1, 1)
-        products(0, 1)
-        round_basis(1, 1, False)
-        round_basis(2, 0, False)
-        quantise_basis(1, 1)
-        products(1, 1)
-        round_basis(2, 1, False)
-        quantise_basis(2, 0)
-        products(2, 0)
-        round_basis(3, 0, False)
-        quantise_basis(2, 1)
-        products(2, 1)
-        round_basis(3, 1, False)
-        quantise_basis(3, 0)
-        products(3, 0)
-        quantise_basis(3, 1)
-        products(3, 1)
-
-        tpl = tile("tpl", [P, PACK, P, 2], U8)
-        nc.vector.tensor_copy(tpl[:], tpl_raw[:].rearrange("p (m t b) -> p t m b", t=PACK, b=2))
-        tpl_sc = tile("tpl_sc", [P, PACK, P], U8)
-        nc.vector.tensor_copy(tpl_sc[:], tpl_raw_scales[:].rearrange("p (m t) -> p t m", t=PACK))
-
-        mags = [tile("mag%d" % i, [P, S], F32) for i in range(PACK)]
-        for i in range(PACK):
-            for jh in range(2):
-                power = bank(2 * i + jh, [P, 4, P])
-                for w in range(2):
-                    for b in range(4):
-                        nc.tensor.matmul(
-                            power[:, b, :],
-                            squares[w, 2 * jh + b // 2][:, b % 2, i, :],
-                            ident[:],
-                            start=(w == 0 and b == 0),
-                            stop=(w == 1 and b == 3),
-                            is_transpose=True,
-                        )
-                nc.scalar.activation(
-                    mags[i][:, jh * BANK : (jh + 1) * BANK], power[:].rearrange("p b j -> p (b j)"), ACT.Sqrt
+            else:
+                nc.tensor.matmul_mx(
+                    out=acc[:],
+                    lhsT=codes[w, a][:, bins].bitcast(FP8X4),
+                    lhsT_scale=scales[w, a][:, bins],
+                    rhs=got_words[a, jh][:].bitcast(FP8X4),
+                    rhs_scale=got_scales[jh][4 * a : P, :],
+                    start=(a == 0),
+                    stop=(a == PASSES - 1),
                 )
 
-        x = [tile("x%d" % mh, [P, PACK, M // 2], F32) for mh in range(2)]
+        def square(w, i, jh):
+            squares[w, i, jh] = tile("squares%d_%d_%d" % (w, i, jh), [P, BANK], F32)
+            nc.scalar.activation(squares[w, i, jh][:], accs[w, i, jh][:], ACT.Square)
 
-        def pick(i, mh):
-            cols = slice(mh * (M // 2), (mh + 1) * (M // 2))
-            entries = picks[:, mh * (M // 2) // LIST_COLS : (mh + 1) * (M // 2) // LIST_COLS]
-            nc.vector.tensor_tensor(x[mh][:, i, :], mags[i][:].indirect(entries), weight[:, cols], MULT)
+        power = {}
 
-        for i, mh in ((0, 0), (0, 1), (1, 0), (1, 1), (2, 0), (3, 0), (2, 1), (3, 1)):
-            pick(i, mh)
+        def turn(w, i, jh):
+            if w == COS:
+                power[i, jh] = bank(2 * i + jh)
+            for u in range(4):
+                cols = slice(u * P, (u + 1) * P)
+                nc.tensor.matmul(
+                    power[i, jh][:, cols],
+                    squares[w, i, jh][:, cols],
+                    ident[:],
+                    start=(w == COS and u == 0),
+                    stop=(w == SIN and u == 3),
+                    is_transpose=True,
+                )
+
+        def add(i, jh):
+            power[i, jh] = tile("power%d_%d" % (i, jh), [P, BANK], F32)
+            nc.vector.tensor_tensor(power[i, jh][:], squares[COS, i, jh][:], squares[SIN, i, jh][:], ADD)
+
+        mags = [tile("mag%d" % i, [P, S], F32) for i in range(PACK)]
+
+        def root(i):
+            for jh in range(2):
+                nc.scalar.activation(mags[i][:, jh * BANK : (jh + 1) * BANK], power[i, jh][:], ACT.Sqrt)
+
+        gather_scales(0)
+        gather_scales(1)
+        round_basis(COS, 0, 0, H // 2, nc.scalar.copy)
+        round_basis(COS, 0, H // 2, H, nc.scalar.copy)
+        quantise_basis(COS, 0, 0, PACK)
+        tpl = tile("tpl", [P, PACK, P, 2], U8)
+        nc.vector.tensor_copy(
+            tpl[:].rearrange("p t m b -> p m t b"), tpl_raw[:].rearrange("p (m t b) -> p m t b", t=PACK, b=2)
+        )
+        for a in range(PASSES):
+            if a == 1:
+                round_basis(COS, 1, 0, H // 2, nc.scalar.copy)
+                round_basis(COS, 1, H // 2, H, nc.scalar.copy)
+                quantise_basis(COS, 1, 0, PACK)
+            for jh in range(2):
+                gather_words(a, jh)
+                for i in range(PACK):
+                    product(COS, i, jh, a, 2 * i + jh)
+                    if a == PASSES - 1:
+                        square(COS, i, jh)
+        sin_grouped = tile("table1", [P, PASSES, PACK, P, PACK], BF16)
+        for a in range(PASSES):
+            grouped[SIN, a] = sin_grouped[:, a]
+        round_basis(SIN, 0, 0, H, nc.vector.tensor_copy)
+        round_basis(SIN, 1, 0, H // 2, nc.vector.tensor_copy)
+        quantise_basis(SIN, 0, 0, 1)
+        round_basis(SIN, 1, H // 2, H, nc.vector.tensor_copy)
+        quantise_basis(SIN, 0, 1, 2)
+        quantise_basis(SIN, 1, 0, 1)
+        quantise_basis(SIN, 0, 2, PACK)
+        quantise_basis(SIN, 1, 1, 2)
+        quantise_basis(SIN, 1, 2, PACK)
+        for jh in range(2):
+            for i in TURNED:
+                turn(COS, i, jh)
+
+        tpl_sc = tile("tpl_sc", [P, PACK, P], U8)
+        nc.vector.tensor_copy(
+            tpl_sc[:].rearrange("p t m -> p m t"), tpl_raw_scales[:].rearrange("p (m t) -> p m t", t=PACK)
+        )
+        x = tile("x", [P, PACK, M], F32)
+
+        def pick(i, m0, m1):
+            entries = picks[:, m0 // LIST_COLS : m1 // LIST_COLS]
+            nc.vector.tensor_tensor(x[:, i, m0:m1], mags[i][:].indirect(entries), weight[:, m0:m1], MULT)
+
+        sin_bank = lambda i, jh: 2 * jh + i % 2
+
+        def sines(i):
+            for a in range(PASSES):
+                for jh in range(2):
+                    product(SIN, i, jh, a, sin_bank(i, jh))
+                    if a == PASSES - 1:
+                        square(SIN, i, jh)
+            for jh in range(2):
+                if i in TURNED:
+                    turn(SIN, i, jh)
+                else:
+                    add(i, jh)
+
+        sines(0)
+        for i in range(PACK):
+            if i + 1 < PACK:
+                sines(i + 1)
+            root(i)
+            if i + 1 < PACK:
+                pick(i, 0, M)
+        pick(PACK - 1, 0, M // 2)
+        pick(PACK - 1, M // 2, M)
 
         z_codes = tile("z_codes", [P, M], U32)
         z_scales = tile("z_scales", [P, M], U8)
         y_codes = tile("y_codes", [P, M], U32)
         y_scales = tile("y_scales", [P, M], U8)
+        y = tile("y", [P, PACK, M], F32)
         y_rows = out_0.rearrange("(p t) m -> p t m", t=PACK)
         y_words = out_1[0].rearrange("p m t -> p (m t)").bitcast(I32)
         z = {}
-        y = {}
         sums = {}
 
         def log_gain(u):
             logs = tile("logs%d" % u, [P, QUARTER, PACK], F32)
-            part = x[u // 2][:, :, (u % 2) * QUARTER : (u % 2 + 1) * QUARTER]
+            part = x[:, :, u * QUARTER : (u + 1) * QUARTER]
             nc.scalar.activation(
                 logs[:].rearrange("p (c e) i -> p c i e", e=4),
                 part.rearrange("p i (c e) -> p c i e", e=4),
@@ -246,10 +288,10 @@ def tile_list_pitch_salience_kernel(
             nc.vector.quantize_mx(
                 out=z_codes[:, cols].bitcast(FP8X4), scales=z_scales[:, cols], in_=z[u][:].rearrange("p m i -> p (m i)")
             )
-            sums[u] = bank(u, [P, PACK, QUARTER])
+            sums[u] = bank(u)
             for t in range(PACK):
                 nc.tensor.matmul_mx(
-                    out=sums[u][:, t, :],
+                    out=sums[u][:, t * QUARTER : (t + 1) * QUARTER],
                     lhsT=tpl[:, t, :, :].rearrange("p m b -> p (m b)").bitcast(FP4X4),
                     lhsT_scale=tpl_sc[:, t, :],
                     rhs=z_codes[:, cols].bitcast(FP8X4),
@@ -260,16 +302,26 @@ def tile_list_pitch_salience_kernel(
 
         def hand_out(u):
             cols = slice(u * QUARTER, (u + 1) * QUARTER)
-            y[u] = tile("y%d" % u, [P, PACK, QUARTER], F32)
-            nc.scalar.copy(y[u][:], sums[u][:])
-            nc.sync.dma_start(y_rows[:, :, cols], y[u][:])
             rounded = tile("rounded%d" % u, [P, QUARTER, PACK], BF16)
-            nc.vector.tensor_copy(
-                rounded[:].rearrange("p (c e) t -> p c t e", e=4), y[u][:].rearrange("p t (c e) -> p c t e", e=4)
-            )
+            if u == 3:
+                nc.vector.tensor_copy(rounded[:], sums[u][:].rearrange("p (t m) -> p m t", t=PACK))
+            nc.scalar.copy(y[:, :, cols], sums[u][:].rearrange("p (t m) -> p t m", t=PACK))
+            if u < 3:
+                nc.vector.tensor_copy(
+                    rounded[:].rearrange("p (c e) t -> p c t e", e=4),
+                    y[:, :, cols].rearrange("p t (c e) -> p c t e", e=4),
+                )
             nc.vector.quantize_mx(
                 out=y_codes[:, cols].bitcast(FP8X4), scales=y_scales[:, cols], in_=rounded[:].rearrange("p m t -> p (m t)")
             )
+
+        def store_values(u0, u1):
+            cols = slice(u0 * QUARTER, u1 * QUARTER)
+            nc.sync.dma_start(y_rows[:, :, cols], y[:, :, cols])
+
+        def store_words(u0, u1):
+            cols = slice(u0 * QUARTER, u1 * QUARTER)
+            nc.sync.dma_start(y_words[:, cols], y_codes[:, cols].bitcast(I32))
 
         log_gain(0)
         log_gain(1)
@@ -278,14 +330,16 @@ def tile_list_pitch_salience_kernel(
         salience(1)
         log_gain(3)
         salience(2)
-        hand_out(0)
         salience(3)
+        hand_out(0)
         hand_out(1)
-        nc.sync.dma_start(y_words[:, 0 : M // 2], y_codes[:, 0 : M // 2].bitcast(I32))
+        store_values(0, 2)
         hand_out(2)
+        store_values(2, 3)
+        store_words(0, 3)
         hand_out(3)
-        nc.sync.dma_start(y_words[:, M // 2 : M], y_codes[:, M // 2 : M].bitcast(I32))
+        store_values(3, 4)
+        store_words(3, 4)
         for q in range(4):
-            nc.scalar.dma_start(
-                out_2[0, 4 * q : 4 * q + 4, :].bitcast(I32), y_scales[32 * q : 32 * q + 4, :].bitcast(I32)
-            )
+            queue = nc.scalar if q % 2 else nc.sync
+            queue.dma_start(out_2[0, 4 * q : 4 * q + 4, :].bitcast(I32), y_scales[32 * q : 32 * q + 4, :].bitcast(I32))

@@ -231,11 +231,12 @@ def tile_list_pitch_salience_kernel(
         nc.vector.tensor_copy(
             tpl_sc[:].rearrange("p t m -> p m t"), tpl_raw_scales[:].rearrange("p (m t) -> p m t", t=PACK)
         )
-        x = tile("x", [P, PACK, M], F32)
+        x = [tile("x%d" % mh, [P, PACK, M // 2], F32) for mh in range(2)]
 
-        def pick(i, m0, m1):
+        def pick(i, mh):
+            m0, m1 = mh * (M // 2), (mh + 1) * (M // 2)
             entries = picks[:, m0 // LIST_COLS : m1 // LIST_COLS]
-            nc.vector.tensor_tensor(x[:, i, m0:m1], mags[i][:].indirect(entries), weight[:, m0:m1], MULT)
+            nc.vector.tensor_tensor(x[mh][:, i, :], mags[i][:].indirect(entries), weight[:, m0:m1], MULT)
 
         sin_bank = lambda i, jh: 2 * jh + i % 2
 
@@ -243,29 +244,39 @@ def tile_list_pitch_salience_kernel(
             for a in range(PASSES):
                 for jh in range(2):
                     product(SIN, i, jh, a, sin_bank(i, jh))
-                    if a == PASSES - 1:
-                        square(SIN, i, jh)
-            for jh in range(2):
-                if i in TURNED:
-                    turn(SIN, i, jh)
-                else:
-                    add(i, jh)
 
-        sines(0)
-        for i in range(PACK):
-            if i + 1 < PACK:
-                sines(i + 1)
+        plain = tile("plain", [P, BANK], F32)
+        for i in range(2):
+            sines(i)
+            for jh in range(2):
+                square(SIN, i, jh)
+        sines(2)
+        sines(3)
+        add(0, 0)
+        add(0, 1)
+        root(0)
+        add(1, 0)
+        nc.vector.tensor_copy(plain[:], accs[SIN, 2, 0][:])
+        add(1, 1)
+        squares[SIN, 2, 0] = tile("squares%d_%d_%d" % (SIN, 2, 0), [P, BANK], F32)
+        nc.vector.tensor_tensor(squares[SIN, 2, 0][:], plain[:], plain[:], MULT)
+        square(SIN, 2, 1)
+        root(1)
+        for jh in range(2):
+            square(SIN, 3, jh)
+        for i in TURNED:
+            for jh in range(2):
+                turn(SIN, i, jh)
             root(i)
-            if i + 1 < PACK:
-                pick(i, 0, M)
-        pick(PACK - 1, 0, M // 2)
-        pick(PACK - 1, M // 2, M)
+        for i in range(PACK):
+            for mh in range(2):
+                pick(i, mh)
 
         z_codes = tile("z_codes", [P, M], U32)
         z_scales = tile("z_scales", [P, M], U8)
         y_codes = tile("y_codes", [P, M], U32)
         y_scales = tile("y_scales", [P, M], U8)
-        y = tile("y", [P, PACK, M], F32)
+        y = [tile("y%d" % u, [P, PACK, QUARTER], F32) for u in range(4)]
         y_rows = out_0.rearrange("(p t) m -> p t m", t=PACK)
         y_words = out_1[0].rearrange("p m t -> p (m t)").bitcast(I32)
         z = {}
@@ -273,14 +284,14 @@ def tile_list_pitch_salience_kernel(
 
         def log_gain(u):
             logs = tile("logs%d" % u, [P, QUARTER, PACK], F32)
-            part = x[:, :, u * QUARTER : (u + 1) * QUARTER]
+            part = x[u // 2][:, :, (u % 2) * QUARTER : (u % 2 + 1) * QUARTER]
             nc.scalar.activation(
                 logs[:].rearrange("p (c e) i -> p c i e", e=4),
                 part.rearrange("p i (c e) -> p c i e", e=4),
                 ACT.Ln,
                 bias=1.0,
             )
-            z[u] = tile("z%d" % u, [P, QUARTER, PACK], BF16)
+            z[u] = tile("z%d" % (1 if u == 3 else u), [P, QUARTER, PACK], BF16)
             nc.vector.tensor_tensor(z[u][:], logs[:], gains[:].unsqueeze(1).to_broadcast([P, QUARTER, PACK]), MULT)
 
         def salience(u):
@@ -300,24 +311,28 @@ def tile_list_pitch_salience_kernel(
                     stop=True,
                 )
 
-        def hand_out(u):
+        rounded = [tile("rounded%d" % u, [P, QUARTER, PACK], BF16) for u in range(4)]
+
+        def copy_out(u):
             cols = slice(u * QUARTER, (u + 1) * QUARTER)
-            rounded = tile("rounded%d" % u, [P, QUARTER, PACK], BF16)
-            if u == 3:
-                nc.vector.tensor_copy(rounded[:], sums[u][:].rearrange("p (t m) -> p m t", t=PACK))
-            nc.scalar.copy(y[:, :, cols], sums[u][:].rearrange("p (t m) -> p t m", t=PACK))
-            if u < 3:
-                nc.vector.tensor_copy(
-                    rounded[:].rearrange("p (c e) t -> p c t e", e=4),
-                    y[:, :, cols].rearrange("p t (c e) -> p c t e", e=4),
-                )
-            nc.vector.quantize_mx(
-                out=y_codes[:, cols].bitcast(FP8X4), scales=y_scales[:, cols], in_=rounded[:].rearrange("p m t -> p (m t)")
+            nc.scalar.copy(y[u][:], sums[u][:].rearrange("p (t m) -> p t m", t=PACK))
+            nc.sync.dma_start(y_rows[:, :, cols], y[u][:])
+
+        def round_copy(u):
+            nc.vector.tensor_copy(
+                rounded[u][:].rearrange("p (c e) t -> p c t e", e=4), y[u][:].rearrange("p t (c e) -> p c t e", e=4)
             )
 
-        def store_values(u0, u1):
-            cols = slice(u0 * QUARTER, u1 * QUARTER)
-            nc.sync.dma_start(y_rows[:, :, cols], y[:, :, cols])
+        def round_sums(u, copy):
+            copy(rounded[u][:], sums[u][:].rearrange("p (t m) -> p m t", t=PACK))
+
+        def quantise_out(u):
+            cols = slice(u * QUARTER, (u + 1) * QUARTER)
+            nc.vector.quantize_mx(
+                out=y_codes[:, cols].bitcast(FP8X4),
+                scales=y_scales[:, cols],
+                in_=rounded[u][:].rearrange("p m t -> p (m t)"),
+            )
 
         def store_words(u0, u1):
             cols = slice(u0 * QUARTER, u1 * QUARTER)
@@ -328,18 +343,23 @@ def tile_list_pitch_salience_kernel(
         salience(0)
         log_gain(2)
         salience(1)
-        log_gain(3)
         salience(2)
+        log_gain(3)
         salience(3)
-        hand_out(0)
-        hand_out(1)
-        store_values(0, 2)
-        hand_out(2)
-        store_values(2, 3)
-        store_words(0, 3)
-        hand_out(3)
-        store_values(3, 4)
-        store_words(3, 4)
+        copy_out(0)
+        round_copy(0)
+        copy_out(1)
+        round_copy(1)
+        quantise_out(0)
+        copy_out(2)
+        round_sums(3, nc.vector.tensor_copy)
+        round_sums(2, nc.scalar.copy)
+        quantise_out(1)
+        store_words(0, 2)
+        copy_out(3)
+        quantise_out(2)
+        quantise_out(3)
+        store_words(2, 4)
         for q in range(4):
             queue = nc.scalar if q % 2 else nc.sync
             queue.dma_start(out_2[0, 4 * q : 4 * q + 4, :].bitcast(I32), y_scales[32 * q : 32 * q + 4, :].bitcast(I32))

@@ -16,7 +16,6 @@ FP8X4 = mybir.dt.float8_e4m3fn_x4
 FP4X4 = mybir.dt.float4_e2m1fn_x4
 ACT = mybir.ActivationFunctionType
 MULT = mybir.AluOpType.mult
-ADD = mybir.AluOpType.add
 
 P = 128
 PACK = 4
@@ -25,7 +24,8 @@ PASSES = K // K_PASS
 BANK = 512
 LIST_COLS = 16
 QUARTER = M // 4
-TURNED = (2, 3)
+CHUNK = H // 2
+GROUPS = 4
 COS, SIN = 0, 1
 
 
@@ -46,8 +46,23 @@ def tile_list_pitch_salience_kernel(
         frames = tile("frames", [P, S // LIST_COLS], U16)
         nc.sync.dma_start(frames[:], offs)
 
+        picks = tile("picks", [P, M // LIST_COLS], U16)
+        nc.sync.dma_start(picks[:], offs2)
+
+        table = [tile("table%d" % a, [P, T], U32) for a in range(PASSES)]
+        basis = (wcos, wsin)
+        raw = {}
+
+        def load_table(a):
+            nc.sync.dma_start(table[a][:].bitcast(I32), tab_words[a].rearrange("p t i -> p (t i)").bitcast(I32))
+
+        def load_basis(w, c, a):
+            raw[w, c, a] = tile("raw%d_%d_%d" % (w, c, a), [P, PACK, CHUNK], F32)
+            rows = basis[w][a * K_PASS : (a + 1) * K_PASS, c * CHUNK : (c + 1) * CHUNK]
+            nc.sync.dma_start(raw[w, c, a][:], rows.rearrange("(p j) c -> p j c", j=PACK))
+
         table_scales = tile("table_scales", [P, T], U8)
-        nc.vector.memset(table_scales[:].bitcast(I32), 0)
+        nc.gpsimd.memset(table_scales[:].bitcast(I32), 0)
         for q in range(4):
             nc.sync.dma_start(
                 table_scales[32 * q : 32 * q + 4 * PASSES, :].bitcast(I32),
@@ -58,32 +73,16 @@ def tile_list_pitch_salience_kernel(
         nc.vector.memset(warm[:, 0:1], 1.0)
         nc.scalar.activation(warm[:, 1:2], warm[:, 0:1], ACT.Sqrt)
 
-        table = [tile("table%d" % a, [P, T], U32) for a in range(PASSES)]
-        basis = (wcos, wsin)
-        raw = {}
+        load_table(0)
+        load_basis(COS, 0, 0)
+        load_basis(COS, 0, 1)
+        load_table(1)
+        for w, c in ((COS, 1), (SIN, 0), (SIN, 1)):
+            for a in range(PASSES):
+                load_basis(w, c, a)
 
-        def load_table(a):
-            nc.sync.dma_start(table[a][:].bitcast(I32), tab_words[a].rearrange("p t i -> p (t i)").bitcast(I32))
-
-        def load_basis(w, a, c0, c1):
-            raw[w, a, c0] = tile("raw%d_%d_%d" % (w, a, c0), [P, PACK, c1 - c0], F32)
-            rows = basis[w][a * K_PASS : (a + 1) * K_PASS, c0:c1]
-            nc.sync.dma_start(raw[w, a, c0][:], rows.rearrange("(p j) c -> p j c", j=PACK))
-
-        load_basis(COS, 0, 0, H // 2)
-        load_basis(COS, 0, H // 2, H)
         tpl_raw = tile("tpl_raw", [P, 2 * N], U8)
         nc.sync.dma_start(tpl_raw[:].bitcast(I32), tpl_words[0].bitcast(I32))
-        load_table(0)
-        load_basis(COS, 1, 0, H // 2)
-        load_basis(COS, 1, H // 2, H)
-        load_table(1)
-        load_basis(SIN, 0, 0, H)
-        load_basis(SIN, 1, 0, H // 2)
-        load_basis(SIN, 1, H // 2, H)
-
-        picks = tile("picks", [P, M // LIST_COLS], U16)
-        nc.sync.dma_start(picks[:], offs2)
         weight = tile("weight", [P, M], F32)
         nc.sync.dma_start(weight[:], wgt)
         gains = tile("gains", [P, PACK], F32)
@@ -100,137 +99,89 @@ def tile_list_pitch_salience_kernel(
         make_identity(nc, ident[:])
 
         got_words = {}
-        got_scales = {}
+        got_scales = tile("got_scales", [P, S], U8)
 
-        def listed(jh):
-            return frames[:, jh * BANK // LIST_COLS : (jh + 1) * BANK // LIST_COLS]
+        def gather_words(a, g0, g1):
+            got = tile("got_words%d_%d" % (a, g0), [P, (g1 - g0) * 2 * P], U32)
+            listed = frames[:, g0 * 2 * P // LIST_COLS : g1 * 2 * P // LIST_COLS]
+            nc.vector.tensor_copy(got[:], table[a][:].indirect(listed))
+            for g in range(g0, g1):
+                got_words[a, g] = got[:, (g - g0) * 2 * P : (g - g0 + 1) * 2 * P]
 
-        def gather_scales(jh):
-            got_scales[jh] = tile("got_scales%d" % jh, [P, BANK], U8)
-            nc.vector.tensor_copy(got_scales[jh][:], table_scales[:].indirect(listed(jh)))
+        grouped = {}
+        codes = {}
+        scales = {}
 
-        def gather_words(a, jh):
-            got_words[a, jh] = tile("got_words%d_%d" % (a, jh), [P, BANK], U32)
-            nc.vector.tensor_copy(got_words[a, jh][:], table[a][:].indirect(listed(jh)))
+        def round_basis(key, copy, c0=0, c1=CHUNK):
+            copy(
+                grouped[key][:, c0:c1, :].rearrange("p (n e) j -> p n j e", e=4),
+                raw[key][:, :, c0:c1].rearrange("p j (n e) -> p n j e", e=4),
+            )
 
-        keys = [(w, a) for w in range(2) for a in range(PASSES)]
-        grouped = {(COS, a): tile("grouped%d" % a, [P, PACK, P, PACK], BF16)[:] for a in range(PASSES)}
-        codes = {k: tile("codes%d_%d" % k, [P, H], U32) for k in keys}
-        scales = {k: tile("scales%d_%d" % k, [P, H], U8) for k in keys}
-
-        def round_basis(w, a, c0, c1, copy, first=None):
-            first = c0 if first is None else first
-            dst = grouped[w, a][:, :, c0 // PACK : c1 // PACK, :].rearrange("p t m j -> p m j t")
-            copy(dst, raw[w, a, first][:, :, c0 - first : c1 - first].rearrange("p j (m t) -> p m j t", t=PACK))
-
-        def quantise_basis(w, a, t0, t1):
+        def quantise_basis(key, c0=0, c1=CHUNK):
+            if c0 == 0:
+                codes[key] = tile("codes%d_%d_%d" % key, [P, CHUNK], U32)
+                scales[key] = tile("scales%d_%d_%d" % key, [P, CHUNK], U8)
             nc.vector.quantize_mx(
-                out=codes[w, a][:, t0 * P : t1 * P].bitcast(FP8X4),
-                scales=scales[w, a][:, t0 * P : t1 * P],
-                in_=grouped[w, a][:, t0:t1, :, :].rearrange("p t m j -> p (t m j)"),
+                out=codes[key][:, c0:c1].bitcast(FP8X4),
+                scales=scales[key][:, c0:c1],
+                in_=grouped[key][:, c0:c1, :].rearrange("p n j -> p (n j)"),
             )
 
         accs = {}
-        squares = {}
+        squares = {
+            (w, g): tile("squares%d_%d" % (w, g), [P, 2, PACK, P], F32) for w in range(2) for g in range(GROUPS)
+        }
 
-        def product(w, i, jh, a, b):
-            bins = slice(i * P, (i + 1) * P)
+        def product(w, c, g, a):
             if a == 0:
-                accs[w, i, jh] = bank(b)
-            acc = accs[w, i, jh]
-            if i in TURNED:
-                for u in range(4):
-                    cols = slice(u * P, (u + 1) * P)
-                    nc.tensor.matmul_mx(
-                        out=acc[:, cols],
-                        lhsT=got_words[a, jh][:, cols].bitcast(FP8X4),
-                        lhsT_scale=got_scales[jh][4 * a : P, cols],
-                        rhs=codes[w, a][:, bins].bitcast(FP8X4),
-                        rhs_scale=scales[w, a][:, bins],
-                        start=(a == 0 and u == 0),
-                        stop=(a == PASSES - 1 and u == 3),
-                    )
-            else:
+                accs[w, c, g] = bank(GROUPS * c + g)
+            for f in range(2):
+                first = (2 * g + f) * P
                 nc.tensor.matmul_mx(
-                    out=acc[:],
-                    lhsT=codes[w, a][:, bins].bitcast(FP8X4),
-                    lhsT_scale=scales[w, a][:, bins],
-                    rhs=got_words[a, jh][:].bitcast(FP8X4),
-                    rhs_scale=got_scales[jh][4 * a : P, :],
-                    start=(a == 0),
-                    stop=(a == PASSES - 1),
+                    out=accs[w, c, g][:, f * CHUNK : (f + 1) * CHUNK],
+                    lhsT=got_words[a, g][:, f * P : (f + 1) * P].bitcast(FP8X4),
+                    lhsT_scale=got_scales[4 * a : P, first : first + P],
+                    rhs=codes[w, c, a][:].bitcast(FP8X4),
+                    rhs_scale=scales[w, c, a][:],
+                    start=(a == 0 and f == 0),
+                    stop=(a == PASSES - 1 and f == 1),
                 )
 
-        def square(w, i, jh):
-            squares[w, i, jh] = tile("squares%d_%d_%d" % (w, i, jh), [P, BANK], F32)
-            nc.scalar.activation(squares[w, i, jh][:], accs[w, i, jh][:], ACT.Square)
+        def dealt(w, c, g):
+            part = CHUNK // PACK
+            return squares[w, g][:, :, :, c * part : (c + 1) * part]
+
+        def square(w, c, g):
+            nc.scalar.activation(
+                dealt(w, c, g), accs[w, c, g][:].rearrange("p (f n i) -> p f i n", f=2, i=PACK), ACT.Square
+            )
+
+        def square_on_vector(w, c, g):
+            plain = tile("plain%d" % g, [P, 2, PACK, CHUNK // PACK], F32)
+            nc.vector.tensor_copy(plain[:], accs[w, c, g][:].rearrange("p (f n i) -> p f i n", f=2, i=PACK))
+            return lambda: nc.vector.tensor_tensor(dealt(w, c, g), plain[:], plain[:], MULT)
 
         power = {}
 
-        def turn(w, i, jh):
+        def turn(w, i, jh, b=None):
             if w == COS:
-                power[i, jh] = bank(2 * i + jh)
+                power[i, jh] = bank(b)
             for u in range(4):
-                cols = slice(u * P, (u + 1) * P)
                 nc.tensor.matmul(
-                    power[i, jh][:, cols],
-                    squares[w, i, jh][:, cols],
+                    power[i, jh][:, u * P : (u + 1) * P],
+                    squares[w, 2 * jh + u // 2][:, u % 2, i, :],
                     ident[:],
                     start=(w == COS and u == 0),
                     stop=(w == SIN and u == 3),
                     is_transpose=True,
                 )
 
-        def add(i, jh):
-            power[i, jh] = tile("power%d_%d" % (i, jh), [P, BANK], F32)
-            nc.vector.tensor_tensor(power[i, jh][:], squares[COS, i, jh][:], squares[SIN, i, jh][:], ADD)
-
         mags = [tile("mag%d" % i, [P, S], F32) for i in range(PACK)]
 
-        def root(i):
-            for jh in range(2):
-                nc.scalar.activation(mags[i][:, jh * BANK : (jh + 1) * BANK], power[i, jh][:], ACT.Sqrt)
+        def root(i, jh):
+            nc.scalar.activation(mags[i][:, jh * BANK : (jh + 1) * BANK], power[i, jh][:], ACT.Sqrt)
 
-        gather_scales(0)
-        gather_scales(1)
-        round_basis(COS, 0, 0, H // 2, nc.scalar.copy)
-        round_basis(COS, 0, H // 2, H, nc.scalar.copy)
-        quantise_basis(COS, 0, 0, PACK)
-        tpl = tile("tpl", [P, PACK, P, 2], U8)
-        nc.vector.tensor_copy(
-            tpl[:].rearrange("p t m b -> p m t b"), tpl_raw[:].rearrange("p (m t b) -> p m t b", t=PACK, b=2)
-        )
-        for a in range(PASSES):
-            if a == 1:
-                round_basis(COS, 1, 0, H // 2, nc.scalar.copy)
-                round_basis(COS, 1, H // 2, H, nc.scalar.copy)
-                quantise_basis(COS, 1, 0, PACK)
-            for jh in range(2):
-                gather_words(a, jh)
-                for i in range(PACK):
-                    product(COS, i, jh, a, 2 * i + jh)
-                    if a == PASSES - 1:
-                        square(COS, i, jh)
-        sin_grouped = tile("table1", [P, PASSES, PACK, P, PACK], BF16)
-        for a in range(PASSES):
-            grouped[SIN, a] = sin_grouped[:, a]
-        round_basis(SIN, 0, 0, H, nc.vector.tensor_copy)
-        round_basis(SIN, 1, 0, H // 2, nc.vector.tensor_copy)
-        quantise_basis(SIN, 0, 0, 1)
-        round_basis(SIN, 1, H // 2, H, nc.vector.tensor_copy)
-        quantise_basis(SIN, 0, 1, 2)
-        quantise_basis(SIN, 1, 0, 1)
-        quantise_basis(SIN, 0, 2, PACK)
-        quantise_basis(SIN, 1, 1, 2)
-        quantise_basis(SIN, 1, 2, PACK)
-        for jh in range(2):
-            for i in TURNED:
-                turn(COS, i, jh)
-
-        tpl_sc = tile("tpl_sc", [P, PACK, P], U8)
-        nc.vector.tensor_copy(
-            tpl_sc[:].rearrange("p t m -> p m t"), tpl_raw_scales[:].rearrange("p (m t) -> p m t", t=PACK)
-        )
         x = [tile("x%d" % mh, [P, PACK, M // 2], F32) for mh in range(2)]
 
         def pick(i, mh):
@@ -238,36 +189,55 @@ def tile_list_pitch_salience_kernel(
             entries = picks[:, m0 // LIST_COLS : m1 // LIST_COLS]
             nc.vector.tensor_tensor(x[mh][:, i, :], mags[i][:].indirect(entries), weight[:, m0:m1], MULT)
 
-        sin_bank = lambda i, jh: 2 * jh + i % 2
-
-        def sines(i):
-            for a in range(PASSES):
-                for jh in range(2):
-                    product(SIN, i, jh, a, sin_bank(i, jh))
-
-        plain = tile("plain", [P, BANK], F32)
-        for i in range(2):
-            sines(i)
-            for jh in range(2):
-                square(SIN, i, jh)
-        sines(2)
-        sines(3)
-        add(0, 0)
-        add(0, 1)
-        root(0)
-        add(1, 0)
-        nc.vector.tensor_copy(plain[:], accs[SIN, 2, 0][:])
-        add(1, 1)
-        squares[SIN, 2, 0] = tile("squares%d_%d_%d" % (SIN, 2, 0), [P, BANK], F32)
-        nc.vector.tensor_tensor(squares[SIN, 2, 0][:], plain[:], plain[:], MULT)
-        square(SIN, 2, 1)
-        root(1)
-        for jh in range(2):
-            square(SIN, 3, jh)
-        for i in TURNED:
-            for jh in range(2):
-                turn(SIN, i, jh)
-            root(i)
+        nc.vector.tensor_copy(got_scales[:], table_scales[:].indirect(frames[:]))
+        gather_words(0, 0, 2)
+        gather_words(0, 2, 4)
+        for a in range(PASSES):
+            grouped[COS, 0, a] = tile("grouped%d" % a, [P, CHUNK, PACK], BF16)[:]
+            round_basis((COS, 0, a), nc.scalar.copy)
+            quantise_basis((COS, 0, a))
+        for g in range(GROUPS):
+            product(COS, 0, g, 0)
+        grouped[COS, 1, 0] = tile("grouped2", [P, CHUNK, PACK], BF16)[:]
+        round_basis((COS, 1, 0), nc.scalar.copy)
+        for g in range(GROUPS):
+            gather_words(1, g, g + 1)
+            product(COS, 0, g, 1)
+            square(COS, 0, g)
+        quantise_basis((COS, 1, 0))
+        for g in range(GROUPS):
+            product(COS, 1, g, 0)
+        later = tile("table1", [P, 5, CHUNK, PACK], BF16)
+        pieces = [(COS, 1, 1), (SIN, 0, 0), (SIN, 0, 1), (SIN, 1, 0), (SIN, 1, 1)]
+        halves = ((0, CHUNK // 2), (CHUNK // 2, CHUNK))
+        for n, key in enumerate(pieces):
+            grouped[key] = later[:, n]
+            for c0, c1 in halves:
+                round_basis(key, nc.vector.tensor_copy, c0, c1)
+            for c0, c1 in halves:
+                quantise_basis(key, c0, c1)
+            w, c, a = key
+            last = n + 1 == len(pieces)
+            for g in (0, 2, 1, 3) if last else range(GROUPS):
+                product(w, c, g, a)
+                if a == 1 and not last:
+                    square(w, c, g)
+        tpl = tile("table1", [P, PACK, P], U16)
+        nc.vector.tensor_copy(tpl[:].rearrange("p t m -> p m t"), tpl_raw[:].bitcast(U16).rearrange("p (m t) -> p m t", t=PACK))
+        square(SIN, 1, 0)
+        later2 = square_on_vector(SIN, 1, 2)
+        tpl_sc = tile("raw1_1_1", [P, PACK, P], U8)
+        nc.vector.tensor_copy(
+            tpl_sc[:].rearrange("p t m -> p m t"), tpl_raw_scales[:].rearrange("p (m t) -> p m t", t=PACK)
+        )
+        later2()
+        square(SIN, 1, 1)
+        square(SIN, 1, 3)
+        order = [(0, 0), (1, 0), (0, 1), (1, 1), (2, 0), (2, 1), (3, 0), (3, 1)]
+        for n, (i, jh) in enumerate(order):
+            turn(COS, i, jh, (0, 1, 2, 3, 4, 6, 5, 7)[n])
+            turn(SIN, i, jh)
+            root(i, jh)
         for i in range(PACK):
             for mh in range(2):
                 pick(i, mh)
@@ -291,7 +261,7 @@ def tile_list_pitch_salience_kernel(
                 ACT.Ln,
                 bias=1.0,
             )
-            z[u] = tile("z%d" % (1 if u == 3 else u), [P, QUARTER, PACK], BF16)
+            z[u] = tile("z%d" % u, [P, QUARTER, PACK], BF16)
             nc.vector.tensor_tensor(z[u][:], logs[:], gains[:].unsqueeze(1).to_broadcast([P, QUARTER, PACK]), MULT)
 
         def salience(u):
@@ -303,7 +273,7 @@ def tile_list_pitch_salience_kernel(
             for t in range(PACK):
                 nc.tensor.matmul_mx(
                     out=sums[u][:, t * QUARTER : (t + 1) * QUARTER],
-                    lhsT=tpl[:, t, :, :].rearrange("p m b -> p (m b)").bitcast(FP4X4),
+                    lhsT=tpl[:, t, :].bitcast(U8).bitcast(FP4X4),
                     lhsT_scale=tpl_sc[:, t, :],
                     rhs=z_codes[:, cols].bitcast(FP8X4),
                     rhs_scale=z_scales[:, cols],
@@ -323,9 +293,6 @@ def tile_list_pitch_salience_kernel(
                 rounded[u][:].rearrange("p (c e) t -> p c t e", e=4), y[u][:].rearrange("p t (c e) -> p c t e", e=4)
             )
 
-        def round_sums(u, copy):
-            copy(rounded[u][:], sums[u][:].rearrange("p (t m) -> p m t", t=PACK))
-
         def quantise_out(u):
             cols = slice(u * QUARTER, (u + 1) * QUARTER)
             nc.vector.quantize_mx(
@@ -343,21 +310,19 @@ def tile_list_pitch_salience_kernel(
         salience(0)
         log_gain(2)
         salience(1)
-        salience(2)
         log_gain(3)
+        salience(2)
         salience(3)
-        copy_out(0)
+        for u in range(4):
+            copy_out(u)
         round_copy(0)
-        copy_out(1)
         round_copy(1)
         quantise_out(0)
-        copy_out(2)
-        round_sums(3, nc.vector.tensor_copy)
-        round_sums(2, nc.scalar.copy)
         quantise_out(1)
         store_words(0, 2)
-        copy_out(3)
+        round_copy(2)
         quantise_out(2)
+        round_copy(3)
         quantise_out(3)
         store_words(2, 4)
         for q in range(4):

@@ -46,9 +46,6 @@ def tile_list_pitch_salience_kernel(
         frames = tile("frames", [P, S // LIST_COLS], U16)
         nc.sync.dma_start(frames[:], offs)
 
-        picks = tile("picks", [P, M // LIST_COLS], U16)
-        nc.sync.dma_start(picks[:], offs2)
-
         table = [tile("table%d" % a, [P, T], U32) for a in range(PASSES)]
         basis = (wcos, wsin)
         raw = {}
@@ -62,8 +59,15 @@ def tile_list_pitch_salience_kernel(
             nc.sync.dma_start(raw[w, c, a][:], rows.rearrange("(p j) c -> p j c", j=PACK))
 
         table_scales = tile("table_scales", [P, T], U8)
-        nc.gpsimd.memset(table_scales[:].bitcast(I32), 0)
-        for q in range(4):
+        nc.gpsimd.memset(table_scales[:, : 3 * T // 4].bitcast(I32), 0)
+        nc.vector.memset(table_scales[:, 3 * T // 4 :].bitcast(I32), 0)
+        for q in range(2):
+            for a in range(PASSES):
+                nc.sync.dma_start(
+                    table_scales[32 * q + 4 * a : 32 * q + 4 * a + 4, :].bitcast(I32),
+                    tab_scales[a, 4 * q : 4 * q + 4, :].bitcast(I32),
+                )
+        for q in range(2, 4):
             nc.sync.dma_start(
                 table_scales[32 * q : 32 * q + 4 * PASSES, :].bitcast(I32),
                 tab_scales[:, 4 * q : 4 * q + 4, :].bitcast(I32),
@@ -75,14 +79,16 @@ def tile_list_pitch_salience_kernel(
 
         load_table(0)
         load_basis(COS, 0, 0)
-        load_basis(COS, 0, 1)
         load_table(1)
+        load_basis(COS, 0, 1)
         for w, c in ((COS, 1), (SIN, 0), (SIN, 1)):
             for a in range(PASSES):
                 load_basis(w, c, a)
 
         tpl_raw = tile("tpl_raw", [P, 2 * N], U8)
         nc.sync.dma_start(tpl_raw[:].bitcast(I32), tpl_words[0].bitcast(I32))
+        picks = tile("picks", [P, M // LIST_COLS], U16)
+        nc.sync.dma_start(picks[:], offs2)
         weight = tile("weight", [P, M], F32)
         nc.sync.dma_start(weight[:], wgt)
         gains = tile("gains", [P, PACK], F32)
@@ -102,7 +108,7 @@ def tile_list_pitch_salience_kernel(
         got_scales = tile("got_scales", [P, S], U8)
 
         def gather_words(a, g0, g1):
-            got = tile("got_words%d_%d" % (a, g0), [P, (g1 - g0) * 2 * P], U32)
+            got = tile("grouped1" if (a, g0) == (1, GROUPS - 1) else "got_words%d_%d" % (a, g0), [P, (g1 - g0) * 2 * P], U32)
             listed = frames[:, g0 * 2 * P // LIST_COLS : g1 * 2 * P // LIST_COLS]
             nc.vector.tensor_copy(got[:], table[a][:].indirect(listed))
             for g in range(g0, g1):
@@ -191,27 +197,28 @@ def tile_list_pitch_salience_kernel(
 
         nc.vector.tensor_copy(got_scales[:], table_scales[:].indirect(frames[:]))
         gather_words(0, 0, 2)
+        for n, key in enumerate(((COS, 0, 0), (COS, 0, 1), (COS, 1, 0))):
+            grouped[key] = tile("grouped%d" % n, [P, CHUNK, PACK], BF16)[:]
+            round_basis(key, nc.scalar.copy)
+        quantise_basis((COS, 0, 0))
         gather_words(0, 2, 4)
-        for a in range(PASSES):
-            grouped[COS, 0, a] = tile("grouped%d" % a, [P, CHUNK, PACK], BF16)[:]
-            round_basis((COS, 0, a), nc.scalar.copy)
-            quantise_basis((COS, 0, a))
         for g in range(GROUPS):
             product(COS, 0, g, 0)
-        grouped[COS, 1, 0] = tile("grouped2", [P, CHUNK, PACK], BF16)[:]
-        round_basis((COS, 1, 0), nc.scalar.copy)
-        for g in range(GROUPS):
+        for g in range(GROUPS - 1):
             gather_words(1, g, g + 1)
+        quantise_basis((COS, 0, 1))
+        gather_words(1, GROUPS - 1, GROUPS)
+        for g in range(GROUPS):
             product(COS, 0, g, 1)
             square(COS, 0, g)
         quantise_basis((COS, 1, 0))
         for g in range(GROUPS):
             product(COS, 1, g, 0)
-        later = tile("table1", [P, 5, CHUNK, PACK], BF16)
+        later = tile("table1", [P, 4, CHUNK, PACK], BF16)
         pieces = [(COS, 1, 1), (SIN, 0, 0), (SIN, 0, 1), (SIN, 1, 0), (SIN, 1, 1)]
         halves = ((0, CHUNK // 2), (CHUNK // 2, CHUNK))
         for n, key in enumerate(pieces):
-            grouped[key] = later[:, n]
+            grouped[key] = later[:, n - 1] if n else tile("grouped2", [P, CHUNK, PACK], BF16)[:]
             for c0, c1 in halves:
                 round_basis(key, nc.vector.tensor_copy, c0, c1)
             for c0, c1 in halves:
@@ -233,7 +240,7 @@ def tile_list_pitch_salience_kernel(
         later2()
         square(SIN, 1, 1)
         square(SIN, 1, 3)
-        order = [(0, 0), (1, 0), (0, 1), (1, 1), (2, 0), (2, 1), (3, 0), (3, 1)]
+        order = [(i, jh) for i in range(PACK) for jh in range(2)]
         for n, (i, jh) in enumerate(order):
             turn(COS, i, jh, (0, 1, 2, 3, 4, 6, 5, 7)[n])
             turn(SIN, i, jh)
@@ -252,17 +259,24 @@ def tile_list_pitch_salience_kernel(
         z = {}
         sums = {}
 
-        def log_gain(u):
+        def log_gain(u, parts=1):
             logs = tile("logs%d" % u, [P, QUARTER, PACK], F32)
-            part = x[u // 2][:, :, (u % 2) * QUARTER : (u % 2 + 1) * QUARTER]
-            nc.scalar.activation(
-                logs[:].rearrange("p (c e) i -> p c i e", e=4),
-                part.rearrange("p i (c e) -> p c i e", e=4),
-                ACT.Ln,
-                bias=1.0,
-            )
             z[u] = tile("z%d" % u, [P, QUARTER, PACK], BF16)
-            nc.vector.tensor_tensor(z[u][:], logs[:], gains[:].unsqueeze(1).to_broadcast([P, QUARTER, PACK]), MULT)
+            width = QUARTER // parts
+            for m0 in range(0, QUARTER, width):
+                first = (u % 2) * QUARTER + m0
+                nc.scalar.activation(
+                    logs[:, m0 : m0 + width, :].rearrange("p (c e) i -> p c i e", e=4),
+                    x[u // 2][:, :, first : first + width].rearrange("p i (c e) -> p c i e", e=4),
+                    ACT.Ln,
+                    bias=1.0,
+                )
+                nc.vector.tensor_tensor(
+                    z[u][:, m0 : m0 + width, :],
+                    logs[:, m0 : m0 + width, :],
+                    gains[:].unsqueeze(1).to_broadcast([P, width, PACK]),
+                    MULT,
+                )
 
         def salience(u):
             cols = slice(u * QUARTER, (u + 1) * QUARTER)
@@ -305,7 +319,7 @@ def tile_list_pitch_salience_kernel(
             cols = slice(u0 * QUARTER, u1 * QUARTER)
             nc.sync.dma_start(y_words[:, cols], y_codes[:, cols].bitcast(I32))
 
-        log_gain(0)
+        log_gain(0, 2)
         log_gain(1)
         salience(0)
         log_gain(2)
@@ -322,9 +336,10 @@ def tile_list_pitch_salience_kernel(
         store_words(0, 2)
         round_copy(2)
         quantise_out(2)
+        store_words(2, 3)
         round_copy(3)
         quantise_out(3)
-        store_words(2, 4)
+        store_words(3, 4)
         for q in range(4):
             queue = nc.scalar if q % 2 else nc.sync
             queue.dma_start(out_2[0, 4 * q : 4 * q + 4, :].bitcast(I32), y_scales[32 * q : 32 * q + 4, :].bitcast(I32))

@@ -38,7 +38,7 @@ def tile_list_pitch_salience_kernel(
         psum = ctx.enter_context(tc.psum_pool(name="psum", bufs=1))
 
         def tile(name, shape, dtype):
-            return keep.tile(shape, dtype, name=name, align_bytes=64)
+            return keep.tile(shape, dtype, name=name, align_bytes=256)
 
         def bank(b):
             return psum.tile([P, BANK], F32, name="bank%d" % b)

@@ -158,15 +158,16 @@ def tile_list_pitch_salience_kernel(
             part = CHUNK // PACK
             return squares[w, g][:, :, :, c * part : (c + 1) * part]
 
-        def square(w, c, g):
-            nc.scalar.activation(
-                dealt(w, c, g), accs[w, c, g][:].rearrange("p (f n i) -> p f i n", f=2, i=PACK), ACT.Square
-            )
+        def planes(w, c, g):
+            return accs[w, c, g][:].rearrange("p (f n i) -> p f i n", f=2, i=PACK)
 
-        def square_on_vector(w, c, g):
-            plain = tile("plain%d" % g, [P, 2, PACK, CHUNK // PACK], F32)
-            nc.vector.tensor_copy(plain[:], accs[w, c, g][:].rearrange("p (f n i) -> p f i n", f=2, i=PACK))
-            return lambda: nc.vector.tensor_tensor(dealt(w, c, g), plain[:], plain[:], MULT)
+        def square(w, c, g, i0=0, i1=PACK):
+            nc.scalar.activation(dealt(w, c, g)[:, :, i0:i1, :], planes(w, c, g)[:, :, i0:i1, :], ACT.Square)
+
+        def square_on_vector(w, c, g, i0=0, i1=PACK):
+            plain = tile("plain%d" % g, [P, 2, i1 - i0, CHUNK // PACK], F32)
+            nc.vector.tensor_copy(plain[:], planes(w, c, g)[:, :, i0:i1, :])
+            return lambda: nc.vector.tensor_tensor(dealt(w, c, g)[:, :, i0:i1, :], plain[:], plain[:], MULT)
 
         power = {}
 
@@ -225,24 +226,24 @@ def tile_list_pitch_salience_kernel(
                 quantise_basis(key, c0, c1)
             w, c, a = key
             last = n + 1 == len(pieces)
-            for g in (0, 2, 1, 3) if last else range(GROUPS):
+            for g in range(GROUPS):
                 product(w, c, g, a)
                 if a == 1 and not last:
                     square(w, c, g)
         tpl = tile("table1", [P, PACK, P], U16)
         nc.vector.tensor_copy(tpl[:].rearrange("p t m -> p m t"), tpl_raw[:].bitcast(U16).rearrange("p (m t) -> p m t", t=PACK))
-        square(SIN, 1, 0)
-        later2 = square_on_vector(SIN, 1, 2)
         tpl_sc = tile("raw1_1_1", [P, PACK, P], U8)
         nc.vector.tensor_copy(
             tpl_sc[:].rearrange("p t m -> p m t"), tpl_raw_scales[:].rearrange("p (m t) -> p m t", t=PACK)
         )
-        later2()
-        square(SIN, 1, 1)
-        square(SIN, 1, 3)
+        for g in range(GROUPS):
+            square(SIN, 1, g, 0, 2)
+        for g0 in (0, 2):
+            for finish in [square_on_vector(SIN, 1, g, 2, PACK) for g in (g0, g0 + 1)]:
+                finish()
         order = [(i, jh) for i in range(PACK) for jh in range(2)]
         for n, (i, jh) in enumerate(order):
-            turn(COS, i, jh, (0, 1, 2, 3, 4, 6, 5, 7)[n])
+            turn(COS, i, jh, n)
             turn(SIN, i, jh)
             root(i, jh)
         for i in range(PACK):
@@ -319,25 +320,28 @@ def tile_list_pitch_salience_kernel(
             cols = slice(u0 * QUARTER, u1 * QUARTER)
             nc.sync.dma_start(y_words[:, cols], y_codes[:, cols].bitcast(I32))
 
+        def round_bank(u):
+            nc.scalar.copy(rounded[u][:], sums[u][:].rearrange("p (t m) -> p m t", t=PACK))
+
         log_gain(0, 2)
-        log_gain(1)
         salience(0)
+        log_gain(1)
         log_gain(2)
         salience(1)
         log_gain(3)
         salience(2)
         salience(3)
-        for u in range(4):
+        for u in range(3):
             copy_out(u)
+        round_bank(3)
+        copy_out(3)
         round_copy(0)
         round_copy(1)
         quantise_out(0)
         quantise_out(1)
-        store_words(0, 2)
         round_copy(2)
         quantise_out(2)
-        store_words(2, 3)
-        round_copy(3)
+        store_words(0, 3)
         quantise_out(3)
         store_words(3, 4)
         for q in range(4):

@@ -320,28 +320,25 @@ def tile_list_pitch_salience_kernel(
             cols = slice(u0 * QUARTER, u1 * QUARTER)
             nc.sync.dma_start(y_words[:, cols], y_codes[:, cols].bitcast(I32))
 
-        def round_bank(u):
-            nc.scalar.copy(rounded[u][:], sums[u][:].rearrange("p (t m) -> p m t", t=PACK))
-
         log_gain(0, 2)
-        salience(0)
         log_gain(1)
+        salience(0)
         log_gain(2)
         salience(1)
         log_gain(3)
         salience(2)
         salience(3)
-        for u in range(3):
+        for u in range(4):
             copy_out(u)
-        round_bank(3)
-        copy_out(3)
         round_copy(0)
         round_copy(1)
         quantise_out(0)
         quantise_out(1)
+        store_words(0, 2)
         round_copy(2)
         quantise_out(2)
-        store_words(0, 3)
+        store_words(2, 3)
+        round_copy(3)
         quantise_out(3)
         store_words(3, 4)
         for q in range(4):

@@ -16,6 +16,7 @@ FP8X4 = mybir.dt.float8_e4m3fn_x4
 FP4X4 = mybir.dt.float4_e2m1fn_x4
 ACT = mybir.ActivationFunctionType
 MULT = mybir.AluOpType.mult
+ADD = mybir.AluOpType.add
 
 P = 128
 PACK = 4
@@ -36,6 +37,10 @@ def tile_list_pitch_salience_kernel(
     with ExitStack() as ctx:
         keep = ctx.enter_context(tc.tile_pool(name="keep", bufs=1))
         psum = ctx.enter_context(tc.psum_pool(name="psum", bufs=1))
+        shared = ctx.enter_context(tc.tile_pool(name="shared", bufs=1))
+
+        def overlaid(name, shape, dtype, offset):
+            return shared.tile(shape, dtype, name=name, align_bytes=256, offset=offset)
 
         def tile(name, shape, dtype):
             return keep.tile(shape, dtype, name=name, align_bytes=256)
@@ -46,7 +51,7 @@ def tile_list_pitch_salience_kernel(
         frames = tile("frames", [P, S // LIST_COLS], U16)
         nc.sync.dma_start(frames[:], offs)
 
-        table = [tile("table%d" % a, [P, T], U32) for a in range(PASSES)]
+        table = [tile("table0", [P, T], U32), overlaid("table1", [P, T], U32, 0)]
         basis = (wcos, wsin)
         raw = {}
 
@@ -215,7 +220,7 @@ def tile_list_pitch_salience_kernel(
         quantise_basis((COS, 1, 0))
         for g in range(GROUPS):
             product(COS, 1, g, 0)
-        later = tile("table1", [P, 4, CHUNK, PACK], BF16)
+        later = overlaid("later", [P, 4, CHUNK, PACK], BF16, 0)
         pieces = [(COS, 1, 1), (SIN, 0, 0), (SIN, 0, 1), (SIN, 1, 0), (SIN, 1, 1)]
         halves = ((0, CHUNK // 2), (CHUNK // 2, CHUNK))
         for n, key in enumerate(pieces):
@@ -230,21 +235,36 @@ def tile_list_pitch_salience_kernel(
                 product(w, c, g, a)
                 if a == 1 and not last:
                     square(w, c, g)
-        tpl = tile("table1", [P, PACK, P], U16)
-        nc.vector.tensor_copy(tpl[:].rearrange("p t m -> p m t"), tpl_raw[:].bitcast(U16).rearrange("p (m t) -> p m t", t=PACK))
-        tpl_sc = tile("raw1_1_1", [P, PACK, P], U8)
-        nc.vector.tensor_copy(
-            tpl_sc[:].rearrange("p t m -> p m t"), tpl_raw_scales[:].rearrange("p (m t) -> p m t", t=PACK)
-        )
+        tpl = overlaid("tpl", [P, PACK, P], U16, 4096)
+        nc.vector.tensor_copy(tpl[:], tpl_raw[:].bitcast(U16).rearrange("p (m t) -> p t m", t=PACK))
+        tpl_sc = overlaid("tpl_sc", [P, PACK, P], U8, 5120)
+        nc.vector.tensor_copy(tpl_sc[:], tpl_raw_scales[:].rearrange("p (m t) -> p t m", t=PACK))
+        summed = [overlaid("summed%d" % g, [P, 2, P], F32, 1024 * g) for g in range(GROUPS)]
+
+        def add_last_plane(c, g):
+            part = slice(c * CHUNK // PACK, (c + 1) * CHUNK // PACK)
+            (nc.vector if c else nc.gpsimd).tensor_tensor(
+                summed[g][:, :, part], dealt(COS, c, g)[:, :, PACK - 1, :], dealt(SIN, c, g)[:, :, PACK - 1, :], ADD
+            )
+
+        for g in range(GROUPS):
+            add_last_plane(0, g)
         for g in range(GROUPS):
             square(SIN, 1, g, 0, 2)
         for g0 in (0, 2):
             for finish in [square_on_vector(SIN, 1, g, 2, PACK) for g in (g0, g0 + 1)]:
                 finish()
+        for g in range(GROUPS):
+            add_last_plane(1, g)
         order = [(i, jh) for i in range(PACK) for jh in range(2)]
         for n, (i, jh) in enumerate(order):
-            turn(COS, i, jh, n)
-            turn(SIN, i, jh)
+            if i < PACK - 1:
+                turn(COS, i, jh, n)
+                turn(SIN, i, jh)
+            else:
+                power[i, jh] = bank(n)
+                for u in range(4):
+                    nc.tensor.transpose(power[i, jh][:, u * P : (u + 1) * P], summed[2 * jh + u // 2][:, u % 2, :], ident[:])
             root(i, jh)
         for i in range(PACK):
             for mh in range(2):

@@ -28,6 +28,9 @@ QUARTER = M // 4
 CHUNK = H // 2
 GROUPS = 4
 COS, SIN = 0, 1
+SINE_RAW = 16384
+LAST_STAGED = SINE_RAW + 2 * 4096
+LAST_RAW = SINE_RAW + 3 * 4096
 
 
 def tile_list_pitch_salience_kernel(
@@ -59,20 +62,16 @@ def tile_list_pitch_salience_kernel(
             nc.sync.dma_start(table[a][:].bitcast(I32), tab_words[a].rearrange("p t i -> p (t i)").bitcast(I32))
 
         def load_basis(w, c, a):
-            raw[w, c, a] = tile("raw%d_%d_%d" % (w, c, a), [P, PACK, CHUNK], F32)
+            name, shape = "raw%d_%d_%d" % (w, c, a), [P, PACK, CHUNK]
+            raw[w, c, a] = overlaid(name, shape, F32, SINE_RAW + 4096 * (2 * c + a)) if w == SIN else tile(name, shape, F32)
             rows = basis[w][a * K_PASS : (a + 1) * K_PASS, c * CHUNK : (c + 1) * CHUNK]
             nc.sync.dma_start(raw[w, c, a][:], rows.rearrange("(p j) c -> p j c", j=PACK))
 
         table_scales = tile("table_scales", [P, T], U8)
         nc.gpsimd.memset(table_scales[:, : 3 * T // 4].bitcast(I32), 0)
         nc.vector.memset(table_scales[:, 3 * T // 4 :].bitcast(I32), 0)
-        for q in range(2):
-            for a in range(PASSES):
-                nc.sync.dma_start(
-                    table_scales[32 * q + 4 * a : 32 * q + 4 * a + 4, :].bitcast(I32),
-                    tab_scales[a, 4 * q : 4 * q + 4, :].bitcast(I32),
-                )
-        for q in range(2, 4):
+        load_table(0)
+        for q in range(4):
             nc.sync.dma_start(
                 table_scales[32 * q : 32 * q + 4 * PASSES, :].bitcast(I32),
                 tab_scales[:, 4 * q : 4 * q + 4, :].bitcast(I32),
@@ -82,13 +81,14 @@ def tile_list_pitch_salience_kernel(
         nc.vector.memset(warm[:, 0:1], 1.0)
         nc.scalar.activation(warm[:, 1:2], warm[:, 0:1], ACT.Sqrt)
 
-        load_table(0)
         load_basis(COS, 0, 0)
-        load_table(1)
+        load_basis(COS, 1, 0)
         load_basis(COS, 0, 1)
-        for w, c in ((COS, 1), (SIN, 0), (SIN, 1)):
+        load_table(1)
+        load_basis(COS, 1, 1)
+        for c in range(2):
             for a in range(PASSES):
-                load_basis(w, c, a)
+                load_basis(SIN, c, a)
 
         tpl_raw = tile("tpl_raw", [P, 2 * N], U8)
         nc.sync.dma_start(tpl_raw[:].bitcast(I32), tpl_words[0].bitcast(I32))
@@ -106,18 +106,25 @@ def tile_list_pitch_salience_kernel(
                 tpl_scales[0, 4 * q : 4 * q + 4, :].bitcast(I32),
             )
 
-        ident = tile("ident", [P, P], F32)
-        make_identity(nc, ident[:])
+        early_ident = tile("early_ident", [P, P], F32)
+        make_identity(nc, early_ident[:])
 
         got_words = {}
-        got_scales = tile("got_scales", [P, S], U8)
+        got_scales = {}
 
-        def gather_words(a, g0, g1):
-            got = tile("grouped1" if (a, g0) == (1, GROUPS - 1) else "got_words%d_%d" % (a, g0), [P, (g1 - g0) * 2 * P], U32)
+        def gather(into, key, window, dtype, g0, g1, offset):
+            name, shape = "got%s_%d" % (key, g0), [P, (g1 - g0) * 2 * P]
+            got = tile(name, shape, dtype) if offset is None else overlaid(name, shape, dtype, offset)
             listed = frames[:, g0 * 2 * P // LIST_COLS : g1 * 2 * P // LIST_COLS]
-            nc.vector.tensor_copy(got[:], table[a][:].indirect(listed))
+            nc.vector.tensor_copy(got[:], window[:].indirect(listed))
             for g in range(g0, g1):
-                got_words[a, g] = got[:, (g - g0) * 2 * P : (g - g0 + 1) * 2 * P]
+                into[key, g] = (got, (g - g0) * 2 * P)
+
+        def gather_words(a, g0, g1, offset=None):
+            gather(got_words, a, table[a], U32, g0, g1, offset)
+
+        def gather_scales(g0, g1, offset=None):
+            gather(got_scales, "s", table_scales, U8, g0, g1, offset)
 
         grouped = {}
         codes = {}
@@ -147,12 +154,13 @@ def tile_list_pitch_salience_kernel(
         def product(w, c, g, a):
             if a == 0:
                 accs[w, c, g] = bank(GROUPS * c + g)
+            words, w0 = got_words[a, g]
+            bytes_, s0 = got_scales["s", g]
             for f in range(2):
-                first = (2 * g + f) * P
                 nc.tensor.matmul_mx(
                     out=accs[w, c, g][:, f * CHUNK : (f + 1) * CHUNK],
-                    lhsT=got_words[a, g][:, f * P : (f + 1) * P].bitcast(FP8X4),
-                    lhsT_scale=got_scales[4 * a : P, first : first + P],
+                    lhsT=words[:, w0 + f * P : w0 + (f + 1) * P].bitcast(FP8X4),
+                    lhsT_scale=bytes_[4 * a : P, s0 + f * P : s0 + (f + 1) * P],
                     rhs=codes[w, c, a][:].bitcast(FP8X4),
                     rhs_scale=scales[w, c, a][:],
                     start=(a == 0 and f == 0),
@@ -201,30 +209,29 @@ def tile_list_pitch_salience_kernel(
             entries = picks[:, m0 // LIST_COLS : m1 // LIST_COLS]
             nc.vector.tensor_tensor(x[mh][:, i, :], mags[i][:].indirect(entries), weight[:, m0:m1], MULT)
 
-        nc.vector.tensor_copy(got_scales[:], table_scales[:].indirect(frames[:]))
-        gather_words(0, 0, 2)
-        for n, key in enumerate(((COS, 0, 0), (COS, 0, 1), (COS, 1, 0))):
-            grouped[key] = tile("grouped%d" % n, [P, CHUNK, PACK], BF16)[:]
+        gather_words(0, 0, 3)
+        gather_scales(0, 2)
+        for n, key in enumerate(((COS, 0, 0), (COS, 1, 0), (COS, 0, 1))):
+            grouped[key] = overlaid("grouped%d" % n, [P, CHUNK, PACK], BF16, 8192 + 2048 * n)[:]
             round_basis(key, nc.scalar.copy)
         quantise_basis((COS, 0, 0))
-        gather_words(0, 2, 4)
-        for g in range(GROUPS):
-            product(COS, 0, g, 0)
-        for g in range(GROUPS - 1):
-            gather_words(1, g, g + 1)
+        gather_scales(2, 3, 8192)
+        gather_words(0, 3, 4, 8192 + 256)
+        quantise_basis((COS, 1, 0))
+        gather_scales(3, 4, 8192 + 2048)
+        for groups in (range(3), range(3, 4)):
+            for c in range(2):
+                for g in groups:
+                    product(COS, c, g, 0)
         quantise_basis((COS, 0, 1))
-        gather_words(1, GROUPS - 1, GROUPS)
         for g in range(GROUPS):
+            gather_words(1, g, g + 1)
             product(COS, 0, g, 1)
             square(COS, 0, g)
-        quantise_basis((COS, 1, 0))
-        for g in range(GROUPS):
-            product(COS, 1, g, 0)
-        later = overlaid("later", [P, 4, CHUNK, PACK], BF16, 0)
         pieces = [(COS, 1, 1), (SIN, 0, 0), (SIN, 0, 1), (SIN, 1, 0), (SIN, 1, 1)]
         halves = ((0, CHUNK // 2), (CHUNK // 2, CHUNK))
         for n, key in enumerate(pieces):
-            grouped[key] = later[:, n - 1] if n else tile("grouped2", [P, CHUNK, PACK], BF16)[:]
+            grouped[key] = overlaid("staged%d" % n, [P, CHUNK, PACK], BF16, SINE_RAW - 2048 if n < 2 else SINE_RAW + 4096 * (n - 2))[:]
             for c0, c1 in halves:
                 round_basis(key, nc.vector.tensor_copy, c0, c1)
             for c0, c1 in halves:
@@ -235,11 +242,13 @@ def tile_list_pitch_salience_kernel(
                 product(w, c, g, a)
                 if a == 1 and not last:
                     square(w, c, g)
-        tpl = overlaid("tpl", [P, PACK, P], U16, 4096)
+        ident = overlaid("ident", [P, P], F32, LAST_RAW)
+        nc.gpsimd.tensor_copy(ident[:], early_ident[:])
+        tpl = overlaid("tpl", [P, PACK, P], U16, LAST_STAGED)
         nc.vector.tensor_copy(tpl[:], tpl_raw[:].bitcast(U16).rearrange("p (m t) -> p t m", t=PACK))
-        tpl_sc = overlaid("tpl_sc", [P, PACK, P], U8, 5120)
+        tpl_sc = overlaid("tpl_sc", [P, PACK, P], U8, LAST_STAGED + 1024)
         nc.vector.tensor_copy(tpl_sc[:], tpl_raw_scales[:].rearrange("p (m t) -> p t m", t=PACK))
-        summed = [overlaid("summed%d" % g, [P, 2, P], F32, 1024 * g) for g in range(GROUPS)]
+        summed = [overlaid("summed%d" % g, [P, 2, P], F32, LAST_RAW + 1024 * (g + 1) if g < GROUPS - 1 else LAST_STAGED + 1536) for g in range(GROUPS)]
 
         def add_last_plane(c, g):
             part = slice(c * CHUNK // PACK, (c + 1) * CHUNK // PACK)

@@ -30,7 +30,6 @@ GROUPS = 4
 COS, SIN = 0, 1
 SINE_RAW = 16384
 LAST_STAGED = SINE_RAW + 2 * 4096
-LAST_RAW = SINE_RAW + 3 * 4096
 
 
 def tile_list_pitch_salience_kernel(
@@ -136,6 +135,9 @@ def tile_list_pitch_salience_kernel(
                 raw[key][:, :, c0:c1].rearrange("p j (n e) -> p n j e", e=4),
             )
 
+        def round_on_gpsimd(out, in_):
+            nc.gpsimd.tensor_scalar(out, in_, 1.0, 0.0, MULT, ADD)
+
         def quantise_basis(key, c0=0, c1=CHUNK):
             if c0 == 0:
                 codes[key] = tile("codes%d_%d_%d" % key, [P, CHUNK], U32)
@@ -233,7 +235,7 @@ def tile_list_pitch_salience_kernel(
         for n, key in enumerate(pieces):
             grouped[key] = overlaid("staged%d" % n, [P, CHUNK, PACK], BF16, SINE_RAW - 2048 if n < 2 else SINE_RAW + 4096 * (n - 2))[:]
             for c0, c1 in halves:
-                round_basis(key, nc.vector.tensor_copy, c0, c1)
+                round_basis(key, nc.vector.tensor_copy if n else round_on_gpsimd, c0, c1)
             for c0, c1 in halves:
                 quantise_basis(key, c0, c1)
             w, c, a = key
@@ -242,38 +244,21 @@ def tile_list_pitch_salience_kernel(
                 product(w, c, g, a)
                 if a == 1 and not last:
                     square(w, c, g)
-        ident = overlaid("ident", [P, P], F32, LAST_RAW)
-        nc.gpsimd.tensor_copy(ident[:], early_ident[:])
+        ident = overlaid("ident", [P, P], F32, LAST_STAGED + 1536)
+        nc.vector.tensor_copy(ident[:], early_ident[:])
         tpl = overlaid("tpl", [P, PACK, P], U16, LAST_STAGED)
         nc.vector.tensor_copy(tpl[:], tpl_raw[:].bitcast(U16).rearrange("p (m t) -> p t m", t=PACK))
         tpl_sc = overlaid("tpl_sc", [P, PACK, P], U8, LAST_STAGED + 1024)
         nc.vector.tensor_copy(tpl_sc[:], tpl_raw_scales[:].rearrange("p (m t) -> p t m", t=PACK))
-        summed = [overlaid("summed%d" % g, [P, 2, P], F32, LAST_RAW + 1024 * (g + 1) if g < GROUPS - 1 else LAST_STAGED + 1536) for g in range(GROUPS)]
-
-        def add_last_plane(c, g):
-            part = slice(c * CHUNK // PACK, (c + 1) * CHUNK // PACK)
-            (nc.vector if c else nc.gpsimd).tensor_tensor(
-                summed[g][:, :, part], dealt(COS, c, g)[:, :, PACK - 1, :], dealt(SIN, c, g)[:, :, PACK - 1, :], ADD
-            )
-
-        for g in range(GROUPS):
-            add_last_plane(0, g)
         for g in range(GROUPS):
             square(SIN, 1, g, 0, 2)
         for g0 in (0, 2):
             for finish in [square_on_vector(SIN, 1, g, 2, PACK) for g in (g0, g0 + 1)]:
                 finish()
-        for g in range(GROUPS):
-            add_last_plane(1, g)
         order = [(i, jh) for i in range(PACK) for jh in range(2)]
         for n, (i, jh) in enumerate(order):
-            if i < PACK - 1:
-                turn(COS, i, jh, n)
-                turn(SIN, i, jh)
-            else:
-                power[i, jh] = bank(n)
-                for u in range(4):
-                    nc.tensor.transpose(power[i, jh][:, u * P : (u + 1) * P], summed[2 * jh + u // 2][:, u % 2, :], ident[:])
+            turn(COS, i, jh, n)
+            turn(SIN, i, jh)
             root(i, jh)
         for i in range(PACK):
             for mh in range(2):

@@ -234,9 +234,10 @@ def tile_list_pitch_salience_kernel(
         halves = ((0, CHUNK // 2), (CHUNK // 2, CHUNK))
         for n, key in enumerate(pieces):
             grouped[key] = overlaid("staged%d" % n, [P, CHUNK, PACK], BF16, SINE_RAW - 2048 if n < 2 else SINE_RAW + 4096 * (n - 2))[:]
-            for c0, c1 in halves:
+            parts = halves if n else ((0, CHUNK),)
+            for c0, c1 in parts:
                 round_basis(key, nc.vector.tensor_copy if n else round_on_gpsimd, c0, c1)
-            for c0, c1 in halves:
+            for c0, c1 in parts:
                 quantise_basis(key, c0, c1)
             w, c, a = key
             last = n + 1 == len(pieces)

@@ -215,7 +215,8 @@ def tile_list_pitch_salience_kernel(
         gather_scales(0, 2)
         for n, key in enumerate(((COS, 0, 0), (COS, 1, 0), (COS, 0, 1))):
             grouped[key] = overlaid("grouped%d" % n, [P, CHUNK, PACK], BF16, 8192 + 2048 * n)[:]
-            round_basis(key, nc.scalar.copy)
+            round_basis(key, nc.scalar.copy, 0, CHUNK // 2)
+            round_basis(key, round_on_gpsimd, CHUNK // 2, CHUNK)
         quantise_basis((COS, 0, 0))
         gather_scales(2, 3, 8192)
         gather_words(0, 3, 4, 8192 + 256)

@@ -81,14 +81,21 @@ def tile_list_pitch_salience_kernel(
         nc.scalar.activation(warm[:, 1:2], warm[:, 0:1], ACT.Sqrt)
 
         load_basis(COS, 0, 0)
-        load_basis(COS, 1, 0)
-        load_basis(COS, 0, 1)
         load_table(1)
+        load_basis(COS, 0, 1)
+        load_basis(COS, 1, 0)
         load_basis(COS, 1, 1)
         for c in range(2):
             for a in range(PASSES):
                 load_basis(SIN, c, a)
 
+        tpl_raw_scales = tile("tpl_raw_scales", [P, N], U8)
+        nc.vector.memset(tpl_raw_scales[:].bitcast(I32), 0)
+        for q in range(4):
+            nc.sync.dma_start(
+                tpl_raw_scales[32 * q : 32 * q + 4, :].bitcast(I32),
+                tpl_scales[0, 4 * q : 4 * q + 4, :].bitcast(I32),
+            )
         tpl_raw = tile("tpl_raw", [P, 2 * N], U8)
         nc.sync.dma_start(tpl_raw[:].bitcast(I32), tpl_words[0].bitcast(I32))
         picks = tile("picks", [P, M // LIST_COLS], U16)
@@ -97,13 +104,6 @@ def tile_list_pitch_salience_kernel(
         nc.sync.dma_start(weight[:], wgt)
         gains = tile("gains", [P, PACK], F32)
         nc.sync.dma_start(gains[:], gain.rearrange("(p i) -> p i", i=PACK))
-        tpl_raw_scales = tile("tpl_raw_scales", [P, N], U8)
-        nc.vector.memset(tpl_raw_scales[:].bitcast(I32), 0)
-        for q in range(4):
-            nc.sync.dma_start(
-                tpl_raw_scales[32 * q : 32 * q + 4, :].bitcast(I32),
-                tpl_scales[0, 4 * q : 4 * q + 4, :].bitcast(I32),
-            )
 
         early_ident = tile("early_ident", [P, P], F32)
         make_identity(nc, early_ident[:])
@@ -204,41 +204,37 @@ def tile_list_pitch_salience_kernel(
         def root(i, jh):
             nc.scalar.activation(mags[i][:, jh * BANK : (jh + 1) * BANK], power[i, jh][:], ACT.Sqrt)
 
-        x = [tile("x%d" % mh, [P, PACK, M // 2], F32) for mh in range(2)]
+        x = tile("x", [P, PACK, M], F32)
 
-        def pick(i, mh):
-            m0, m1 = mh * (M // 2), (mh + 1) * (M // 2)
+        def pick(i, m0, m1):
             entries = picks[:, m0 // LIST_COLS : m1 // LIST_COLS]
-            nc.vector.tensor_tensor(x[mh][:, i, :], mags[i][:].indirect(entries), weight[:, m0:m1], MULT)
+            nc.vector.tensor_tensor(x[:, i, m0:m1], mags[i][:].indirect(entries), weight[:, m0:m1], MULT)
 
-        gather_words(0, 0, 3)
-        gather_scales(0, 2)
-        for n, key in enumerate(((COS, 0, 0), (COS, 1, 0), (COS, 0, 1))):
-            grouped[key] = overlaid("grouped%d" % n, [P, CHUNK, PACK], BF16, 8192 + 2048 * n)[:]
-            round_basis(key, nc.scalar.copy, 0, CHUNK // 2)
-            round_basis(key, round_on_gpsimd, CHUNK // 2, CHUNK)
-        quantise_basis((COS, 0, 0))
-        gather_scales(2, 3, 8192)
-        gather_words(0, 3, 4, 8192 + 256)
-        quantise_basis((COS, 1, 0))
-        gather_scales(3, 4, 8192 + 2048)
-        for groups in (range(3), range(3, 4)):
-            for c in range(2):
-                for g in groups:
-                    product(COS, c, g, 0)
-        quantise_basis((COS, 0, 1))
-        for g in range(GROUPS):
-            gather_words(1, g, g + 1)
-            product(COS, 0, g, 1)
-            square(COS, 0, g)
-        pieces = [(COS, 1, 1), (SIN, 0, 0), (SIN, 0, 1), (SIN, 1, 0), (SIN, 1, 1)]
         halves = ((0, CHUNK // 2), (CHUNK // 2, CHUNK))
+        early = [(COS, 0, 0), (COS, 0, 1), (COS, 1, 0)]
+        for n, key in enumerate(early):
+            grouped[key] = overlaid("grouped%d" % n, [P, CHUNK, PACK], BF16, 8192 + 2048 * n)[:]
+            for copy, (c0, c1) in zip((nc.scalar.copy, round_on_gpsimd), halves):
+                round_basis(key, copy, c0, c1)
+        gather_words(0, 0, GROUPS)
+        gather_scales(0, 2)
+        quantise_basis(early[0])
+        gather_scales(2, GROUPS, 8192)
+        gather_words(1, 0, 3)
+        quantise_basis(early[1])
+        gather_words(1, 3, GROUPS, 8192 + 2048)
+        quantise_basis(early[2])
+        for w, c, a in early:
+            for g in range(GROUPS):
+                product(w, c, g, a)
+                if a == 1:
+                    square(w, c, g)
+        pieces = [(COS, 1, 1), (SIN, 0, 0), (SIN, 0, 1), (SIN, 1, 0), (SIN, 1, 1)]
         for n, key in enumerate(pieces):
-            grouped[key] = overlaid("staged%d" % n, [P, CHUNK, PACK], BF16, SINE_RAW - 2048 if n < 2 else SINE_RAW + 4096 * (n - 2))[:]
-            parts = halves if n else ((0, CHUNK),)
-            for c0, c1 in parts:
-                round_basis(key, nc.vector.tensor_copy if n else round_on_gpsimd, c0, c1)
-            for c0, c1 in parts:
+            grouped[key] = overlaid("staged%d" % n, [P, CHUNK, PACK], BF16, 8192 + 2048 * (n + 2) if n < 2 else SINE_RAW + 4096 * (n - 2))[:]
+            for c0, c1 in halves:
+                round_basis(key, nc.vector.tensor_copy, c0, c1)
+            for c0, c1 in halves:
                 quantise_basis(key, c0, c1)
             w, c, a = key
             last = n + 1 == len(pieces)
@@ -262,9 +258,10 @@ def tile_list_pitch_salience_kernel(
             turn(COS, i, jh, n)
             turn(SIN, i, jh)
             root(i, jh)
-        for i in range(PACK):
-            for mh in range(2):
-                pick(i, mh)
+        for i in range(PACK - 1):
+            pick(i, 0, M)
+        pick(PACK - 1, 0, M // 2)
+        pick(PACK - 1, M // 2, M)
 
         z_codes = tile("z_codes", [P, M], U32)
         z_scales = tile("z_scales", [P, M], U8)
@@ -281,10 +278,10 @@ def tile_list_pitch_salience_kernel(
             z[u] = tile("z%d" % u, [P, QUARTER, PACK], BF16)
             width = QUARTER // parts
             for m0 in range(0, QUARTER, width):
-                first = (u % 2) * QUARTER + m0
+                first = u * QUARTER + m0
                 nc.scalar.activation(
                     logs[:, m0 : m0 + width, :].rearrange("p (c e) i -> p c i e", e=4),
-                    x[u // 2][:, :, first : first + width].rearrange("p i (c e) -> p c i e", e=4),
+                    x[:, :, first : first + width].rearrange("p i (c e) -> p c i e", e=4),
                     ACT.Ln,
                     bias=1.0,
                 )

@@ -30,6 +30,7 @@ GROUPS = 4
 COS, SIN = 0, 1
 SINE_RAW = 16384
 LAST_STAGED = SINE_RAW + 2 * 4096
+TEMPLATE_RAW = SINE_RAW + 4 * 4096
 
 
 def tile_list_pitch_salience_kernel(
@@ -51,7 +52,6 @@ def tile_list_pitch_salience_kernel(
             return psum.tile([P, BANK], F32, name="bank%d" % b)
 
         frames = tile("frames", [P, S // LIST_COLS], U16)
-        nc.sync.dma_start(frames[:], offs)
 
         table = [tile("table0", [P, T], U32), overlaid("table1", [P, T], U32, 0)]
         basis = (wcos, wsin)
@@ -70,6 +70,7 @@ def tile_list_pitch_salience_kernel(
         nc.gpsimd.memset(table_scales[:, : 3 * T // 4].bitcast(I32), 0)
         nc.vector.memset(table_scales[:, 3 * T // 4 :].bitcast(I32), 0)
         load_table(0)
+        nc.sync.dma_start(frames[:], offs)
         for q in range(4):
             nc.sync.dma_start(
                 table_scales[32 * q : 32 * q + 4 * PASSES, :].bitcast(I32),
@@ -89,14 +90,14 @@ def tile_list_pitch_salience_kernel(
             for a in range(PASSES):
                 load_basis(SIN, c, a)
 
-        tpl_raw_scales = tile("tpl_raw_scales", [P, N], U8)
+        tpl_raw_scales = overlaid("tpl_raw_scales", [P, N], U8, TEMPLATE_RAW + 2 * N)
         nc.vector.memset(tpl_raw_scales[:].bitcast(I32), 0)
         for q in range(4):
             nc.sync.dma_start(
                 tpl_raw_scales[32 * q : 32 * q + 4, :].bitcast(I32),
                 tpl_scales[0, 4 * q : 4 * q + 4, :].bitcast(I32),
             )
-        tpl_raw = tile("tpl_raw", [P, 2 * N], U8)
+        tpl_raw = overlaid("tpl_raw", [P, 2 * N], U8, TEMPLATE_RAW)
         nc.sync.dma_start(tpl_raw[:].bitcast(I32), tpl_words[0].bitcast(I32))
         picks = tile("picks", [P, M // LIST_COLS], U16)
         nc.sync.dma_start(picks[:], offs2)
@@ -180,9 +181,8 @@ def tile_list_pitch_salience_kernel(
             nc.scalar.activation(dealt(w, c, g)[:, :, i0:i1, :], planes(w, c, g)[:, :, i0:i1, :], ACT.Square)
 
         def square_on_vector(w, c, g, i0=0, i1=PACK):
-            plain = tile("plain%d" % g, [P, 2, i1 - i0, CHUNK // PACK], F32)
-            nc.vector.tensor_copy(plain[:], planes(w, c, g)[:, :, i0:i1, :])
-            return lambda: nc.vector.tensor_tensor(dealt(w, c, g)[:, :, i0:i1, :], plain[:], plain[:], MULT)
+            nc.vector.tensor_copy(plain[:, g], planes(w, c, g)[:, :, i0:i1, :])
+            return lambda: nc.vector.tensor_tensor(dealt(w, c, g)[:, :, i0:i1, :], plain[:, g], plain[:, g], MULT)
 
         power = {}
 
@@ -250,6 +250,7 @@ def tile_list_pitch_salience_kernel(
         nc.vector.tensor_copy(tpl_sc[:], tpl_raw_scales[:].rearrange("p (m t) -> p t m", t=PACK))
         for g in range(GROUPS):
             square(SIN, 1, g, 0, 2)
+        plain = overlaid("plain", [P, GROUPS, 2, 2, CHUNK // PACK], F32, TEMPLATE_RAW)
         for g0 in (0, 2):
             for finish in [square_on_vector(SIN, 1, g, 2, PACK) for g in (g0, g0 + 1)]:
                 finish()

@@ -132,8 +132,8 @@ def tile_list_pitch_salience_kernel(
 
         def round_basis(key, copy, c0=0, c1=CHUNK):
             copy(
-                grouped[key][:, c0:c1, :].rearrange("p (n e) j -> p n j e", e=4),
-                raw[key][:, :, c0:c1].rearrange("p j (n e) -> p n j e", e=4),
+                grouped[key][:, c0:c1, :].rearrange("p (n e) j -> p n j e", e=2),
+                raw[key][:, :, c0:c1].rearrange("p j (n e) -> p n j e", e=2),
             )
 
         def round_on_gpsimd(out, in_):
@@ -281,8 +281,8 @@ def tile_list_pitch_salience_kernel(
             for m0 in range(0, QUARTER, width):
                 first = u * QUARTER + m0
                 nc.scalar.activation(
-                    logs[:, m0 : m0 + width, :].rearrange("p (c e) i -> p c i e", e=4),
-                    x[:, :, first : first + width].rearrange("p i (c e) -> p c i e", e=4),
+                    logs[:, m0 : m0 + width, :].rearrange("p (c e) i -> p c i e", e=2),
+                    x[:, :, first : first + width].rearrange("p i (c e) -> p c i e", e=2),
                     ACT.Ln,
                     bias=1.0,
                 )
@@ -319,7 +319,7 @@ def tile_list_pitch_salience_kernel(
 
         def round_copy(u):
             nc.vector.tensor_copy(
-                rounded[u][:].rearrange("p (c e) t -> p c t e", e=4), y[u][:].rearrange("p t (c e) -> p c t e", e=4)
+                rounded[u][:].rearrange("p (c e) t -> p c t e", e=2), y[u][:].rearrange("p t (c e) -> p c t e", e=2)
             )
 
         def quantise_out(u):

@@ -150,9 +150,8 @@ def tile_list_pitch_salience_kernel(
             )
 
         accs = {}
-        squares = {
-            (w, g): tile("squares%d_%d" % (w, g), [P, 2, PACK, P], F32) for w in range(2) for g in range(GROUPS)
-        }
+        all_squares = [tile("squares%d" % w, [P, 2 * GROUPS, PACK, P], F32) for w in range(2)]
+        squares = {(w, g): all_squares[w][:, 2 * g : 2 * g + 2] for w in range(2) for g in range(GROUPS)}
 
         def product(w, c, g, a):
             if a == 0:
@@ -180,22 +179,23 @@ def tile_list_pitch_salience_kernel(
         def square(w, c, g, i0=0, i1=PACK):
             nc.scalar.activation(dealt(w, c, g)[:, :, i0:i1, :], planes(w, c, g)[:, :, i0:i1, :], ACT.Square)
 
-        def square_on_vector(w, c, g, i0=0, i1=PACK):
-            nc.vector.tensor_copy(plain[:, g], planes(w, c, g)[:, :, i0:i1, :])
-            return lambda: nc.vector.tensor_tensor(dealt(w, c, g)[:, :, i0:i1, :], plain[:, g], plain[:, g], MULT)
+        def square_on_vector(slot, w, c, g, i0, i1):
+            nc.vector.tensor_copy(plain[:, slot], planes(w, c, g)[:, :, i0:i1, :])
+            return lambda: nc.vector.tensor_tensor(dealt(w, c, g)[:, :, i0:i1, :], plain[:, slot], plain[:, slot], MULT)
 
         power = {}
 
         def turn(w, i, jh, b=None):
-            if w == COS:
+            opens = b is not None
+            if opens:
                 power[i, jh] = bank(b)
             for u in range(4):
                 nc.tensor.matmul(
                     power[i, jh][:, u * P : (u + 1) * P],
                     squares[w, 2 * jh + u // 2][:, u % 2, i, :],
                     ident[:],
-                    start=(w == COS and u == 0),
-                    stop=(w == SIN and u == 3),
+                    start=(opens and u == 0),
+                    stop=(not opens and u == 3),
                     is_transpose=True,
                 )
 
@@ -203,8 +203,6 @@ def tile_list_pitch_salience_kernel(
 
         def root(i, jh):
             nc.scalar.activation(mags[i][:, jh * BANK : (jh + 1) * BANK], power[i, jh][:], ACT.Sqrt)
-
-        x = tile("x", [P, PACK, M], F32)
 
         def pick(i, m0, m1):
             entries = picks[:, m0 // LIST_COLS : m1 // LIST_COLS]
@@ -248,17 +246,30 @@ def tile_list_pitch_salience_kernel(
         nc.vector.tensor_copy(tpl[:], tpl_raw[:].bitcast(U16).rearrange("p (m t) -> p t m", t=PACK))
         tpl_sc = overlaid("tpl_sc", [P, PACK, P], U8, LAST_STAGED + 1024)
         nc.vector.tensor_copy(tpl_sc[:], tpl_raw_scales[:].rearrange("p (m t) -> p t m", t=PACK))
+        plain = overlaid("plain", [P, GROUPS, 2, 2, CHUNK // PACK], F32, TEMPLATE_RAW)
+        finishes = [square_on_vector(g, SIN, 1, g, 2, PACK) for g in range(GROUPS)]
         for g in range(GROUPS):
             square(SIN, 1, g, 0, 2)
-        plain = overlaid("plain", [P, GROUPS, 2, 2, CHUNK // PACK], F32, TEMPLATE_RAW)
-        for g0 in (0, 2):
-            for finish in [square_on_vector(SIN, 1, g, 2, PACK) for g in (g0, g0 + 1)]:
-                finish()
+        for finish in finishes:
+            finish()
+        summed = overlaid("summed", [P, 2 * GROUPS, P], F32, TEMPLATE_RAW - 2048)
+        for c in range(2):
+            bins = slice(c * CHUNK // PACK, (c + 1) * CHUNK // PACK)
+            nc.vector.tensor_tensor(
+                summed[:, :, bins], all_squares[COS][:, :, PACK - 1, bins], all_squares[SIN][:, :, PACK - 1, bins], ADD
+            )
         order = [(i, jh) for i in range(PACK) for jh in range(2)]
         for n, (i, jh) in enumerate(order):
-            turn(COS, i, jh, n)
-            turn(SIN, i, jh)
+            if i == PACK - 1:
+                power[i, jh] = bank(n)
+                for u in range(4):
+                    nc.tensor.transpose(power[i, jh][:, u * P : (u + 1) * P], summed[:, 4 * jh + u, :], ident[:])
+            else:
+                first, second = (SIN, COS) if i == 1 else (COS, SIN)
+                turn(first, i, jh, n)
+                turn(second, i, jh)
             root(i, jh)
+        x = overlaid("x", [P, PACK, M], F32, TEMPLATE_RAW + 2048)
         for i in range(PACK - 1):
             pick(i, 0, M)
         pick(PACK - 1, 0, M // 2)

@@ -30,7 +30,7 @@ GROUPS = 4
 COS, SIN = 0, 1
 SINE_RAW = 16384
 LAST_STAGED = SINE_RAW + 2 * 4096
-TEMPLATE_RAW = SINE_RAW + 4 * 4096
+TEMPLATE_RAW = SINE_RAW + 4 * 4096 + 512
 
 
 def tile_list_pitch_salience_kernel(
@@ -90,7 +90,7 @@ def tile_list_pitch_salience_kernel(
             for a in range(PASSES):
                 load_basis(SIN, c, a)
 
-        tpl_raw_scales = overlaid("tpl_raw_scales", [P, N], U8, TEMPLATE_RAW + 2 * N)
+        tpl_raw_scales = overlaid("tpl_raw_scales", [P, N], U8, TEMPLATE_RAW - N)
         nc.vector.memset(tpl_raw_scales[:].bitcast(I32), 0)
         for q in range(4):
             nc.sync.dma_start(
@@ -244,19 +244,19 @@ def tile_list_pitch_salience_kernel(
         nc.vector.tensor_copy(ident[:], early_ident[:])
         tpl = overlaid("tpl", [P, PACK, P], U16, LAST_STAGED)
         nc.vector.tensor_copy(tpl[:], tpl_raw[:].bitcast(U16).rearrange("p (m t) -> p t m", t=PACK))
-        tpl_sc = overlaid("tpl_sc", [P, PACK, P], U8, LAST_STAGED + 1024)
-        nc.vector.tensor_copy(tpl_sc[:], tpl_raw_scales[:].rearrange("p (m t) -> p t m", t=PACK))
-        plain = overlaid("plain", [P, GROUPS, 2, 2, CHUNK // PACK], F32, TEMPLATE_RAW)
+        tpl_sc = overlaid("tpl_sc", [P, PACK, P], U8, TEMPLATE_RAW)
+        nc.gpsimd.tensor_copy(tpl_sc[:], tpl_raw_scales[:].rearrange("p (m t) -> p t m", t=PACK))
+        plain = overlaid("plain", [P, GROUPS, 2, 2, CHUNK // PACK], F32, TEMPLATE_RAW + 512)
         finishes = [square_on_vector(g, SIN, 1, g, 2, PACK) for g in range(GROUPS)]
         for g in range(GROUPS):
             square(SIN, 1, g, 0, 2)
         for finish in finishes:
             finish()
-        summed = overlaid("summed", [P, 2 * GROUPS, P], F32, TEMPLATE_RAW - 2048)
-        for c in range(2):
-            bins = slice(c * CHUNK // PACK, (c + 1) * CHUNK // PACK)
+        summed = tile("summed", [P, 2 * GROUPS, P], F32)
+        for jh in range(2):
+            tiles = slice(jh * GROUPS, (jh + 1) * GROUPS)
             nc.vector.tensor_tensor(
-                summed[:, :, bins], all_squares[COS][:, :, PACK - 1, bins], all_squares[SIN][:, :, PACK - 1, bins], ADD
+                summed[:, tiles], all_squares[COS][:, tiles, PACK - 1], all_squares[SIN][:, tiles, PACK - 1], ADD
             )
         order = [(i, jh) for i in range(PACK) for jh in range(2)]
         for n, (i, jh) in enumerate(order):

@@ -279,7 +279,7 @@ def tile_list_pitch_salience_kernel(
         z_scales = tile("z_scales", [P, M], U8)
         y_codes = tile("y_codes", [P, M], U32)
         y_scales = tile("y_scales", [P, M], U8)
-        y = [tile("y%d" % u, [P, PACK, QUARTER], F32) for u in range(4)]
+        y = tile("y", [P, PACK, M], F32)
         y_rows = out_0.rearrange("(p t) m -> p t m", t=PACK)
         y_words = out_1[0].rearrange("p m t -> p (m t)").bitcast(I32)
         z = {}
@@ -321,16 +321,21 @@ def tile_list_pitch_salience_kernel(
                     stop=True,
                 )
 
-        rounded = [tile("rounded%d" % u, [P, QUARTER, PACK], BF16) for u in range(4)]
+        rounded = tile("rounded", [P, M, PACK], BF16)
 
-        def copy_out(u):
+        def copy_out(u, parts):
             cols = slice(u * QUARTER, (u + 1) * QUARTER)
-            nc.scalar.copy(y[u][:], sums[u][:].rearrange("p (t m) -> p t m", t=PACK))
-            nc.sync.dma_start(y_rows[:, :, cols], y[u][:])
+            planes_of_bank = sums[u][:].rearrange("p (t m) -> p t m", t=PACK)
+            width = QUARTER // parts
+            for m0 in range(0, QUARTER, width):
+                first = u * QUARTER + m0
+                nc.scalar.copy(y[:, :, first : first + width], planes_of_bank[:, :, m0 : m0 + width])
+            nc.sync.dma_start(y_rows[:, :, cols], y[:, :, cols])
 
-        def round_copy(u):
+        def round_copy(m0, m1):
             nc.vector.tensor_copy(
-                rounded[u][:].rearrange("p (c e) t -> p c t e", e=2), y[u][:].rearrange("p t (c e) -> p c t e", e=2)
+                rounded[:, m0:m1, :].rearrange("p (c e) t -> p c t e", e=2),
+                y[:, :, m0:m1].rearrange("p t (c e) -> p c t e", e=2),
             )
 
         def quantise_out(u):
@@ -338,7 +343,7 @@ def tile_list_pitch_salience_kernel(
             nc.vector.quantize_mx(
                 out=y_codes[:, cols].bitcast(FP8X4),
                 scales=y_scales[:, cols],
-                in_=rounded[u][:].rearrange("p m t -> p (m t)"),
+                in_=rounded[:, cols, :].rearrange("p m t -> p (m t)"),
             )
 
         def store_words(u0, u1):
@@ -354,16 +359,17 @@ def tile_list_pitch_salience_kernel(
         salience(2)
         salience(3)
         for u in range(4):
-            copy_out(u)
-        round_copy(0)
-        round_copy(1)
+            copy_out(u, 2 if u == 3 else 1)
+        round_copy(0, 128)
+        round_copy(128, 256)
         quantise_out(0)
         quantise_out(1)
         store_words(0, 2)
-        round_copy(2)
+        round_copy(256, 368)
+        round_copy(368, 448)
+        round_copy(448, 512)
         quantise_out(2)
         store_words(2, 3)
-        round_copy(3)
         quantise_out(3)
         store_words(3, 4)
         for q in range(4):

from contextlib import ExitStack

import concourse.mybir as mybir
from concourse.masks import make_identity

K, T, S, M, H, N = 1024, 2048, 1024, 512, 512, 512
FLOPS = 2 * (2 * K * H * S) + 2 * H * N * M

F32 = mybir.dt.float32
BF16 = mybir.dt.bfloat16
I32 = mybir.dt.int32
U32 = mybir.dt.uint32
U16 = mybir.dt.uint16
U8 = mybir.dt.uint8
FP8X4 = mybir.dt.float8_e4m3fn_x4
FP4X4 = mybir.dt.float4_e2m1fn_x4
ACT = mybir.ActivationFunctionType
MULT = mybir.AluOpType.mult
ADD = mybir.AluOpType.add

P = 128
PACK = 4
K_PASS = P * PACK
PASSES = K // K_PASS
BANK = 512
LIST_COLS = 16
QUARTER = M // 4
CHUNK = H // 2
GROUPS = 4
COS, SIN = 0, 1
SINE_RAW = 16384
LAST_STAGED = SINE_RAW + 2 * 4096
TEMPLATE_RAW = SINE_RAW + 4 * 4096 + 512


def tile_list_pitch_salience_kernel(
    tc, tab_words, tab_scales, offs, wcos, wsin, offs2, wgt, gain, tpl_words, tpl_scales, out_0, out_1, out_2
):
    nc = tc.nc
    with ExitStack() as ctx:
        keep = ctx.enter_context(tc.tile_pool(name="keep", bufs=1))
        psum = ctx.enter_context(tc.psum_pool(name="psum", bufs=1))
        shared = ctx.enter_context(tc.tile_pool(name="shared", bufs=1))

        def overlaid(name, shape, dtype, offset):
            return shared.tile(shape, dtype, name=name, align_bytes=256, offset=offset)

        def tile(name, shape, dtype):
            return keep.tile(shape, dtype, name=name, align_bytes=256)

        def bank(b):
            return psum.tile([P, BANK], F32, name="bank%d" % b)

        frames = tile("frames", [P, S // LIST_COLS], U16)

        table = [tile("table0", [P, T], U32), overlaid("table1", [P, T], U32, 0)]
        basis = (wcos, wsin)
        raw = {}

        def load_table(a):
            nc.sync.dma_start(table[a][:].bitcast(I32), tab_words[a].rearrange("p t i -> p (t i)").bitcast(I32))

        def load_basis(w, c, a):
            name, shape = "raw%d_%d_%d" % (w, c, a), [P, PACK, CHUNK]
            raw[w, c, a] = overlaid(name, shape, F32, SINE_RAW + 4096 * (2 * c + a)) if w == SIN else tile(name, shape, F32)
            rows = basis[w][a * K_PASS : (a + 1) * K_PASS, c * CHUNK : (c + 1) * CHUNK]
            nc.sync.dma_start(raw[w, c, a][:], rows.rearrange("(p j) c -> p j c", j=PACK))

        table_scales = tile("table_scales", [P, T], U8)
        nc.gpsimd.memset(table_scales[:, : 3 * T // 4].bitcast(I32), 0)
        nc.vector.memset(table_scales[:, 3 * T // 4 :].bitcast(I32), 0)
        load_table(0)
        nc.sync.dma_start(frames[:], offs)
        for q in range(4):
            nc.sync.dma_start(
                table_scales[32 * q : 32 * q + 4 * PASSES, :].bitcast(I32),
                tab_scales[:, 4 * q : 4 * q + 4, :].bitcast(I32),
            )

        warm = tile("warm", [P, 2], F32)
        nc.vector.memset(warm[:, 0:1], 1.0)
        nc.scalar.activation(warm[:, 1:2], warm[:, 0:1], ACT.Sqrt)

        load_basis(COS, 0, 0)
        load_table(1)
        load_basis(COS, 0, 1)
        load_basis(COS, 1, 0)
        load_basis(COS, 1, 1)
        for c in range(2):
            for a in range(PASSES):
                load_basis(SIN, c, a)

        tpl_raw_scales = overlaid("tpl_raw_scales", [P, N], U8, TEMPLATE_RAW - N)
        nc.vector.memset(tpl_raw_scales[:].bitcast(I32), 0)
        for q in range(4):
            nc.sync.dma_start(
                tpl_raw_scales[32 * q : 32 * q + 4, :].bitcast(I32),
                tpl_scales[0, 4 * q : 4 * q + 4, :].bitcast(I32),
            )
        tpl_raw = overlaid("tpl_raw", [P, 2 * N], U8, TEMPLATE_RAW)
        nc.sync.dma_start(tpl_raw[:].bitcast(I32), tpl_words[0].bitcast(I32))
        picks = tile("picks", [P, M // LIST_COLS], U16)
        nc.sync.dma_start(picks[:], offs2)
        weight = tile("weight", [P, M], F32)
        nc.sync.dma_start(weight[:], wgt)
        gains = tile("gains", [P, PACK], F32)
        nc.sync.dma_start(gains[:], gain.rearrange("(p i) -> p i", i=PACK))

        early_ident = tile("early_ident", [P, P], F32)
        make_identity(nc, early_ident[:])

        got_words = {}
        got_scales = {}

        def gather(into, key, window, dtype, g0, g1, offset):
            name, shape = "got%s_%d" % (key, g0), [P, (g1 - g0) * 2 * P]
            got = tile(name, shape, dtype) if offset is None else overlaid(name, shape, dtype, offset)
            listed = frames[:, g0 * 2 * P // LIST_COLS : g1 * 2 * P // LIST_COLS]
            nc.vector.tensor_copy(got[:], window[:].indirect(listed))
            for g in range(g0, g1):
                into[key, g] = (got, (g - g0) * 2 * P)

        def gather_words(a, g0, g1, offset=None):
            gather(got_words, a, table[a], U32, g0, g1, offset)

        def gather_scales(g0, g1, offset=None):
            gather(got_scales, "s", table_scales, U8, g0, g1, offset)

        grouped = {}
        codes = {}
        scales = {}

        def round_basis(key, copy, c0=0, c1=CHUNK):
            copy(
                grouped[key][:, c0:c1, :].rearrange("p (n e) j -> p n j e", e=2),
                raw[key][:, :, c0:c1].rearrange("p j (n e) -> p n j e", e=2),
            )

        def round_on_gpsimd(out, in_):
            nc.gpsimd.tensor_scalar(out, in_, 1.0, 0.0, MULT, ADD)

        def quantise_basis(key, c0=0, c1=CHUNK):
            if c0 == 0:
                codes[key] = tile("codes%d_%d_%d" % key, [P, CHUNK], U32)
                scales[key] = tile("scales%d_%d_%d" % key, [P, CHUNK], U8)
            nc.vector.quantize_mx(
                out=codes[key][:, c0:c1].bitcast(FP8X4),
                scales=scales[key][:, c0:c1],
                in_=grouped[key][:, c0:c1, :].rearrange("p n j -> p (n j)"),
            )

        accs = {}
        all_squares = [tile("squares%d" % w, [P, 2 * GROUPS, PACK, P], F32) for w in range(2)]
        squares = {(w, g): all_squares[w][:, 2 * g : 2 * g + 2] for w in range(2) for g in range(GROUPS)}

        def product(w, c, g, a):
            if a == 0:
                accs[w, c, g] = bank(GROUPS * c + g)
            words, w0 = got_words[a, g]
            bytes_, s0 = got_scales["s", g]
            for f in range(2):
                nc.tensor.matmul_mx(
                    out=accs[w, c, g][:, f * CHUNK : (f + 1) * CHUNK],
                    lhsT=words[:, w0 + f * P : w0 + (f + 1) * P].bitcast(FP8X4),
                    lhsT_scale=bytes_[4 * a : P, s0 + f * P : s0 + (f + 1) * P],
                    rhs=codes[w, c, a][:].bitcast(FP8X4),
                    rhs_scale=scales[w, c, a][:],
                    start=(a == 0 and f == 0),
                    stop=(a == PASSES - 1 and f == 1),
                )

        def dealt(w, c, g):
            part = CHUNK // PACK
            return squares[w, g][:, :, :, c * part : (c + 1) * part]

        def planes(w, c, g):
            return accs[w, c, g][:].rearrange("p (f n i) -> p f i n", f=2, i=PACK)

        def square(w, c, g, i0=0, i1=PACK):
            nc.scalar.activation(dealt(w, c, g)[:, :, i0:i1, :], planes(w, c, g)[:, :, i0:i1, :], ACT.Square)

        def square_on_vector(slot, w, c, g, i0, i1):
            nc.vector.tensor_copy(plain[:, slot], planes(w, c, g)[:, :, i0:i1, :])
            return lambda: nc.vector.tensor_tensor(dealt(w, c, g)[:, :, i0:i1, :], plain[:, slot], plain[:, slot], MULT)

        power = {}

        def turn(w, i, jh, b=None):
            opens = b is not None
            if opens:
                power[i, jh] = bank(b)
            for u in range(4):
                nc.tensor.matmul(
                    power[i, jh][:, u * P : (u + 1) * P],
                    squares[w, 2 * jh + u // 2][:, u % 2, i, :],
                    ident[:],
                    start=(opens and u == 0),
                    stop=(not opens and u == 3),
                    is_transpose=True,
                )

        mags = [tile("mag%d" % i, [P, S], F32) for i in range(PACK)]

        def root(i, jh):
            nc.scalar.activation(mags[i][:, jh * BANK : (jh + 1) * BANK], power[i, jh][:], ACT.Sqrt)

        def pick(i, m0, m1):
            entries = picks[:, m0 // LIST_COLS : m1 // LIST_COLS]
            nc.vector.tensor_tensor(x[:, i, m0:m1], mags[i][:].indirect(entries), weight[:, m0:m1], MULT)

        halves = ((0, CHUNK // 2), (CHUNK // 2, CHUNK))
        early = [(COS, 0, 0), (COS, 0, 1), (COS, 1, 0)]
        for n, key in enumerate(early):
            grouped[key] = overlaid("grouped%d" % n, [P, CHUNK, PACK], BF16, 8192 + 2048 * n)[:]
            for copy, (c0, c1) in zip((nc.scalar.copy, round_on_gpsimd), halves):
                round_basis(key, copy, c0, c1)
        gather_words(0, 0, GROUPS)
        gather_scales(0, 2)
        quantise_basis(early[0])
        gather_scales(2, GROUPS, 8192)
        gather_words(1, 0, 3)
        quantise_basis(early[1])
        gather_words(1, 3, GROUPS, 8192 + 2048)
        quantise_basis(early[2])
        for w, c, a in early:
            for g in range(GROUPS):
                product(w, c, g, a)
                if a == 1:
                    square(w, c, g)
        pieces = [(COS, 1, 1), (SIN, 0, 0), (SIN, 0, 1), (SIN, 1, 0), (SIN, 1, 1)]
        for n, key in enumerate(pieces):
            grouped[key] = overlaid("staged%d" % n, [P, CHUNK, PACK], BF16, 8192 + 2048 * (n + 2) if n < 2 else SINE_RAW + 4096 * (n - 2))[:]
            for c0, c1 in halves:
                round_basis(key, nc.vector.tensor_copy, c0, c1)
            for c0, c1 in halves:
                quantise_basis(key, c0, c1)
            w, c, a = key
            last = n + 1 == len(pieces)
            for g in range(GROUPS):
                product(w, c, g, a)
                if a == 1 and not last:
                    square(w, c, g)
        ident = overlaid("ident", [P, P], F32, LAST_STAGED + 1536)
        nc.vector.tensor_copy(ident[:], early_ident[:])
        tpl = overlaid("tpl", [P, PACK, P], U16, LAST_STAGED)
        nc.vector.tensor_copy(tpl[:], tpl_raw[:].bitcast(U16).rearrange("p (m t) -> p t m", t=PACK))
        tpl_sc = overlaid("tpl_sc", [P, PACK, P], U8, TEMPLATE_RAW)
        nc.gpsimd.tensor_copy(tpl_sc[:], tpl_raw_scales[:].rearrange("p (m t) -> p t m", t=PACK))
        plain = overlaid("plain", [P, GROUPS, 2, 2, CHUNK // PACK], F32, TEMPLATE_RAW + 512)
        finishes = [square_on_vector(g, SIN, 1, g, 2, PACK) for g in range(GROUPS)]
        for g in range(GROUPS):
            square(SIN, 1, g, 0, 2)
        for finish in finishes:
            finish()
        summed = tile("summed", [P, 2 * GROUPS, P], F32)
        for jh in range(2):
            tiles = slice(jh * GROUPS, (jh + 1) * GROUPS)
            nc.vector.tensor_tensor(
                summed[:, tiles], all_squares[COS][:, tiles, PACK - 1], all_squares[SIN][:, tiles, PACK - 1], ADD
            )
        order = [(i, jh) for i in range(PACK) for jh in range(2)]
        for n, (i, jh) in enumerate(order):
            if i == PACK - 1:
                power[i, jh] = bank(n)
                for u in range(4):
                    nc.tensor.transpose(power[i, jh][:, u * P : (u + 1) * P], summed[:, 4 * jh + u, :], ident[:])
            else:
                first, second = (SIN, COS) if i == 1 else (COS, SIN)
                turn(first, i, jh, n)
                turn(second, i, jh)
            root(i, jh)
        x = overlaid("x", [P, PACK, M], F32, TEMPLATE_RAW + 2048)
        for i in range(PACK - 1):
            pick(i, 0, M)
        pick(PACK - 1, 0, M // 2)
        pick(PACK - 1, M // 2, M)

        z_codes = tile("z_codes", [P, M], U32)
        z_scales = tile("z_scales", [P, M], U8)
        y_codes = tile("y_codes", [P, M], U32)
        y_scales = tile("y_scales", [P, M], U8)
        y = tile("y", [P, PACK, M], F32)
        y_rows = out_0.rearrange("(p t) m -> p t m", t=PACK)
        y_words = out_1[0].rearrange("p m t -> p (m t)").bitcast(I32)
        z = {}
        sums = {}

        def log_gain(u, parts=1):
            logs = tile("logs%d" % u, [P, QUARTER, PACK], F32)
            z[u] = tile("z%d" % u, [P, QUARTER, PACK], BF16)
            width = QUARTER // parts
            for m0 in range(0, QUARTER, width):
                first = u * QUARTER + m0
                nc.scalar.activation(
                    logs[:, m0 : m0 + width, :].rearrange("p (c e) i -> p c i e", e=2),
                    x[:, :, first : first + width].rearrange("p i (c e) -> p c i e", e=2),
                    ACT.Ln,
                    bias=1.0,
                )
                nc.vector.tensor_tensor(
                    z[u][:, m0 : m0 + width, :],
                    logs[:, m0 : m0 + width, :],
                    gains[:].unsqueeze(1).to_broadcast([P, width, PACK]),
                    MULT,
                )

        def salience(u):
            cols = slice(u * QUARTER, (u + 1) * QUARTER)
            nc.vector.quantize_mx(
                out=z_codes[:, cols].bitcast(FP8X4), scales=z_scales[:, cols], in_=z[u][:].rearrange("p m i -> p (m i)")
            )
            sums[u] = bank(u)
            for t in range(PACK):
                nc.tensor.matmul_mx(
                    out=sums[u][:, t * QUARTER : (t + 1) * QUARTER],
                    lhsT=tpl[:, t, :].bitcast(U8).bitcast(FP4X4),
                    lhsT_scale=tpl_sc[:, t, :],
                    rhs=z_codes[:, cols].bitcast(FP8X4),
                    rhs_scale=z_scales[:, cols],
                    start=True,
                    stop=True,
                )

        rounded = tile("rounded", [P, M, PACK], BF16)

        def copy_out(u, parts):
            cols = slice(u * QUARTER, (u + 1) * QUARTER)
            planes_of_bank = sums[u][:].rearrange("p (t m) -> p t m", t=PACK)
            width = QUARTER // parts
            for m0 in range(0, QUARTER, width):
                first = u * QUARTER + m0
                nc.scalar.copy(y[:, :, first : first + width], planes_of_bank[:, :, m0 : m0 + width])
            nc.sync.dma_start(y_rows[:, :, cols], y[:, :, cols])

        def round_copy(m0, m1):
            nc.vector.tensor_copy(
                rounded[:, m0:m1, :].rearrange("p (c e) t -> p c t e", e=2),
                y[:, :, m0:m1].rearrange("p t (c e) -> p c t e", e=2),
            )

        def quantise_out(u):
            cols = slice(u * QUARTER, (u + 1) * QUARTER)
            nc.vector.quantize_mx(
                out=y_codes[:, cols].bitcast(FP8X4),
                scales=y_scales[:, cols],
                in_=rounded[:, cols, :].rearrange("p m t -> p (m t)"),
            )

        def store_words(u0, u1):
            cols = slice(u0 * QUARTER, u1 * QUARTER)
            nc.sync.dma_start(y_words[:, cols], y_codes[:, cols].bitcast(I32))

        log_gain(0, 2)
        log_gain(1)
        salience(0)
        log_gain(2)
        salience(1)
        log_gain(3)
        salience(2)
        salience(3)
        for u in range(4):
            copy_out(u, 2 if u == 3 else 1)
        round_copy(0, 128)
        round_copy(128, 256)
        quantise_out(0)
        quantise_out(1)
        store_words(0, 2)
        round_copy(256, 368)
        round_copy(368, 448)
        round_copy(448, 512)
        quantise_out(2)
        store_words(2, 3)
        quantise_out(3)
        store_words(3, 4)
        for q in range(4):
            queue = nc.scalar if q % 2 else nc.sync
            queue.dma_start(out_2[0, 4 * q : 4 * q + 4, :].bitcast(I32), y_scales[32 * q : 32 * q + 4, :].bitcast(I32))
